import numpy as np
import ml_dtypes


def mxq(x, axis, fmt="e4m3"):
    dtype, down = {"e4m3": (ml_dtypes.float8_e4m3fn, 7), "e5m2": (ml_dtypes.float8_e5m2, 14)}[fmt]
    v = np.moveaxis(np.asarray(x, np.float32).astype(ml_dtypes.bfloat16).astype(np.float64), axis, -1)
    blocks = v.reshape(v.shape[:-1] + (-1, 32))
    amax = np.abs(blocks).max(-1, keepdims=True)
    byte = np.maximum(np.where(amax > 0, np.frexp(amax)[1] - 1 + 127, 0) - down, 1)
    scale = np.exp2(byte - 127.0)
    codes = (blocks / scale).astype(np.float32).astype(dtype).astype(np.float64)
    return np.moveaxis((codes * scale).reshape(v.shape), -1, axis)


WIDE = False


def mx_kscale(k):
    if not WIDE:
        return np.ones(k)
    levels = np.array([24, -24, 12, -12, 0])
    if k % 512:
        return np.exp2(np.random.permutation(np.resize(levels, k // 32))).repeat(32)
    a = np.empty((k // 512, 16))
    for p in range(k // 512):
        a[p, :8] = np.random.permutation(np.resize(levels, 8))
        for g in range(8):
            far = levels[np.abs(levels - a[p, g]) >= 10]
            a[p, g + 8] = far[np.random.randint(len(far))]
    return np.exp2(a.ravel()).repeat(32)


def f64(x):
    return np.asarray(x).astype(np.float64)


def striped(idx):
    return np.tile(idx.reshape(-1, 16).T, (8, 1)).astype(np.uint16)


def unstriped(offs):
    return offs[:16].T.reshape(-1).astype(np.int64)


E2M1 = np.array([0.0, 0.5, 1.0, 1.5, 2.0, 3.0, 4.0, 6.0, -0.0, -0.5, -1.0, -1.5, -2.0, -3.0, -4.0, -6.0])


def pack_weight(w, fmt):
    k, n = w.shape
    w = f64(np.asarray(w, np.float32).astype(ml_dtypes.bfloat16)).reshape(k // 32, 32, n)
    amax = np.abs(w).max(1)
    if fmt == "e4m3":
        byte = np.frexp(amax)[1] - 1 + 127 - 7
    else:
        mant, ex = np.frexp(amax / 6.0)
        byte = np.where(mant > 0.5, ex, ex - 1) + 127
    byte = np.clip(np.where(amax > 0, byte, 1), 1, 254)
    scaled = (w * np.exp2(127.0 - byte)[:, None, :]).reshape(k, n).astype(np.float32)
    by_word = np.ascontiguousarray(scaled.reshape(k // 512, 128, 4, n).transpose(0, 1, 3, 2))
    if fmt == "e4m3":
        words = by_word.astype(ml_dtypes.float8_e4m3fn).view(np.uint8)
    else:
        c = by_word.astype(ml_dtypes.float4_e2m1fn).view(np.uint8) & 0xF
        words = (c[..., 0::2] | (c[..., 1::2] << 4)).reshape(k // 512, 128, 2 * n)
    return np.ascontiguousarray(words), np.ascontiguousarray(byte.astype(np.uint8).reshape(k // 512, 16, n))


def unpack_weight(words, scales, fmt):
    g, _, n = scales.shape
    words = np.ascontiguousarray(words).reshape(g, 128, n, -1)
    if fmt == "e4m3":
        vals = words.view(ml_dtypes.float8_e4m3fn).astype(np.float64)
    else:
        nib = np.empty((g, 128, n, 4), np.uint8)
        nib[..., 0::2] = words & 0xF
        nib[..., 1::2] = words >> 4
        vals = E2M1[nib]
    vals = vals * np.repeat(np.exp2(scales.astype(np.float64) - 127.0), 8, axis=1)[..., None]
    return vals.transpose(0, 1, 3, 2).reshape(g * 512, n)


def split(x):
    m, e = np.frexp(f64(x))
    hi = np.ldexp(np.trunc(16.0 * m) / 16.0, e)
    return hi, f64(x) - hi


def sigm(f):
    return 1.0 / (1.0 + np.exp(-np.maximum(f, -700.0)))


def gelu(f):
    return 0.5 * f * (1.0 + np.tanh(np.sqrt(2.0 / np.pi) * (f + 0.044715 * f**3)))


K, N, T, J = 512, 256, 1024, 512


def setup_inputs():
    n = np.random.standard_normal
    s = mx_kscale(K)[:, None]
    p_tab = pack_weight(n((K, T)) * s, "e4m3")
    p_wg = pack_weight(n((K, N)) / np.sqrt(K) / s, "e2m1")
    return {
        "tab_words": p_tab[0],
        "tab_scales": p_tab[1],
        "wg_words": p_wg[0],
        "wg_scales": p_wg[1],
        "wh": (n((K, N)) / np.sqrt(K) / s).astype(np.float32),
        "bg": (0.3 * n(N) - 1.0).astype(np.float32),
        "rT": (n((N, T))).astype(np.float32),
        "offs": striped(np.random.permutation(T)[:J]),
    }


def reference(tab_words, tab_scales, wg_words, wg_scales, wh, bg, rT, offs):
    idx = unstriped(offs)
    tab_ = unpack_weight(tab_words, tab_scales, "e4m3")[:, idx]
    wg_ = unpack_weight(wg_words, wg_scales, "e2m1")
    wh_hi, wh_lo = split(wh)
    wh_hi_, wh_lo_ = mxq(wh_hi, 0, "e4m3"), mxq(wh_lo, 0, "e4m3")
    ga = wg_.T @ tab_
    gate = sigm(ga + f64(bg)[:, None])
    ha = wh_hi_.T @ tab_ + wh_lo_.T @ tab_
    return f64(rT)[:, idx] + gate * (gelu(ha) - f64(rT)[:, idx])

@@ -1,0 +1,143 @@
+from contextlib import ExitStack
+
+import concourse.mybir as mybir
+
+K, N, T, J = 512, 256, 1024, 512
+FLOPS = 3 * 2 * K * N * J
+
+F32 = mybir.dt.float32
+BF16 = mybir.dt.bfloat16
+I32 = mybir.dt.int32
+U32 = mybir.dt.uint32
+U16 = mybir.dt.uint16
+U8 = mybir.dt.uint8
+FP8X4 = mybir.dt.float8_e4m3fn_x4
+FP4X4 = mybir.dt.float4_e2m1fn_x4
+ALU = mybir.AluOpType
+ACT = mybir.ActivationFunctionType
+
+P = 128
+PACK = 4
+TILES = N // P
+HI_MASK_PAIR = 0xFFF0FFF0 - (1 << 32)
+
+
+def load_scale_rows(queue, plane, rows):
+    words = rows.bitcast(I32)
+    width = words.shape[1]
+    for q in range(4):
+        quad = words[4 * q : 4 * q + 4, :].unsqueeze(0).to_broadcast([8, 4, width])
+        queue.dma_start(out=plane[32 * q : 32 * q + 32, :].bitcast(I32), in_=quad)
+
+
+def tile_list_hwayt_hl_gelu_kernel(
+    tc, tab_words, tab_scales, wg_words, wg_scales, wh, bg, rT, offs, out
+):
+    nc = tc.nc
+    with ExitStack() as ctx:
+        sb = ctx.enter_context(tc.tile_pool(name="sb", bufs=1))
+        ps = ctx.enter_context(tc.psum_pool(name="ps", bufs=1))
+
+        offsets = sb.tile([P, J // 16], U16, name="offsets")
+        tab_plane = sb.tile([P, T], U8, name="tab_plane", align_bytes=64)
+        tab_codes = sb.tile([P, T], U32, name="tab_codes", align_bytes=64)
+        wg_plane = sb.tile([P, N], U8, name="wg_plane", align_bytes=64)
+        wg_codes = sb.tile([P, 2 * N], U8, name="wg_codes", align_bytes=64)
+        bias = sb.tile([P, TILES], F32, name="bias")
+        half_bias = sb.tile([P, TILES], F32, name="half_bias")
+        warm = sb.tile([P, 1], F32, name="warm")
+        warm_out = sb.tile([P, 1], F32, name="warm_out")
+        w_raw = [sb.tile([P, PACK, P], F32, name="w_raw%d" % u, align_bytes=64) for u in range(TILES)]
+        r_rows = [sb.tile([P, T], F32, name="r_rows%d" % u, align_bytes=64) for u in range(TILES)]
+
+        nc.gpsimd.memset(warm[:], 0.0)
+        nc.scalar.activation(warm_out[:], warm[:], ACT.Gelu_apprx_tanh)
+
+        nc.sync.dma_start(offsets[:], offs)
+        load_scale_rows(nc.sync, tab_plane, tab_scales[0])
+        nc.sync.dma_start(out=tab_codes[:].bitcast(I32), in_=tab_words[0].rearrange("p t i -> p (t i)").bitcast(I32))
+        wh_rows = wh.rearrange("(p i) n -> p i n", i=PACK)
+        for u in range(TILES):
+            nc.sync.dma_start(out=w_raw[u][:], in_=wh_rows[:, :, u * P : (u + 1) * P])
+        nc.sync.dma_start(out=wg_codes[:].bitcast(I32), in_=wg_words[0].bitcast(I32))
+        load_scale_rows(nc.sync, wg_plane, wg_scales[0])
+        with nc.allow_non_contiguous_dma(reason="one bias value a partition"):
+            nc.sync.dma_start(out=bias[:], in_=bg.rearrange("(u p) -> p u", p=P))
+        for u in range(TILES):
+            nc.sync.dma_start(out=r_rows[u][:], in_=rT[u * P : (u + 1) * P, :])
+
+        v_plane = sb.tile([P, J], U8, name="v_plane", align_bytes=64)
+        v_codes = sb.tile([P, J], U32, name="v_codes", align_bytes=64)
+        nc.vector.tensor_copy(v_plane[:], tab_plane[:].indirect(offsets[:]))
+        nc.vector.tensor_copy(v_codes[:], tab_codes[:].indirect(offsets[:]))
+
+        nc.scalar.mul(half_bias[:], bias[:], 0.5)
+
+        w_codes, w_plane = [], []
+        for u in range(TILES):
+            upper = sb.tile([P, P, PACK], BF16, name="upper%d" % u, align_bytes=64)
+            parts = sb.tile([P, 2 * P * PACK], BF16, name="parts%d" % u, align_bytes=64)
+            codes = sb.tile([P, 2 * P], U32, name="w_codes%d" % u, align_bytes=64)
+            plane = sb.tile([P, 2 * P], U8, name="w_plane%d" % u, align_bytes=64)
+            halves = w_raw[u][:].bitcast(BF16).rearrange("p i (n h) -> p n i h", h=2)
+            nc.scalar.copy(upper[:], halves[:, :, :, 1])
+            hi = parts[:, 0 : P * PACK]
+            lo = parts[:, P * PACK : 2 * P * PACK]
+            nc.vector.tensor_single_scalar(
+                hi.bitcast(I32), upper[:].rearrange("p n i -> p (n i)").bitcast(I32), HI_MASK_PAIR, ALU.bitwise_and
+            )
+            nc.vector.tensor_tensor(
+                lo.rearrange("p (n i) -> p n i", i=PACK),
+                w_raw[u][:].rearrange("p i n -> p n i"),
+                hi.rearrange("p (n i) -> p n i", i=PACK),
+                ALU.subtract,
+            )
+            nc.vector.quantize_mx(out=codes[:].bitcast(FP8X4), scales=plane[:], in_=parts[:])
+            w_codes.append(codes)
+            w_plane.append(plane)
+
+        tanhs, gelus = [], []
+        for u in range(TILES):
+            ga = ps.tile([P, J], F32, name="ga%d" % u)
+            nc.tensor.matmul_mx(
+                out=ga[:],
+                lhsT=wg_codes[:, 2 * u * P : 2 * (u + 1) * P].bitcast(FP4X4),
+                lhsT_scale=wg_plane[:, u * P : (u + 1) * P],
+                rhs=v_codes[:].bitcast(FP8X4),
+                rhs_scale=v_plane[:],
+                start=True,
+                stop=True,
+            )
+            th = sb.tile([P, J], F32, name="tanh%d" % u, align_bytes=64)
+            nc.scalar.activation(th[:], ga[:], ACT.Tanh, bias=half_bias[:, u : u + 1], scale=0.5)
+            tanhs.append(th)
+        for u in range(TILES):
+            ha = ps.tile([P, J], F32, name="ha%d" % u)
+            for part in range(2):
+                cols = slice(part * P, (part + 1) * P)
+                nc.tensor.matmul_mx(
+                    out=ha[:],
+                    lhsT=w_codes[u][:, cols].bitcast(FP8X4),
+                    lhsT_scale=w_plane[u][:, cols],
+                    rhs=v_codes[:].bitcast(FP8X4),
+                    rhs_scale=v_plane[:],
+                    start=(part == 0),
+                    stop=(part == 1),
+                )
+            h = sb.tile([P, J], F32, name="gelu%d" % u, align_bytes=64)
+            nc.scalar.activation(h[:], ha[:], ACT.Gelu_apprx_tanh)
+            gelus.append(h)
+
+        diffs, scaled = [], []
+        for u in range(TILES):
+            d = sb.tile([P, J], F32, name="diff%d" % u, align_bytes=64)
+            nc.vector.tensor_tensor(d[:], r_rows[u][:].indirect(offsets[:]), gelus[u][:], ALU.subtract)
+            diffs.append(d)
+        for u in range(TILES):
+            e = sb.tile([P, J], F32, name="scaled%d" % u, align_bytes=64)
+            nc.vector.scalar_tensor_tensor(e[:], tanhs[u][:], 1.0, diffs[u][:], ALU.subtract, ALU.mult)
+            scaled.append(e)
+        for u in range(TILES):
+            o = sb.tile([P, J], F32, name="result%d" % u, align_bytes=64)
+            nc.vector.scalar_tensor_tensor(o[:], scaled[u][:], -0.5, gelus[u][:], ALU.mult, ALU.add)
+            nc.sync.dma_start(out=out[u * P : (u + 1) * P, :], in_=o[:])

@@ -22,12 +22,12 @@ TILES = N // P
 HI_MASK_PAIR = 0xFFF0FFF0 - (1 << 32)
 
 
-def load_scale_rows(queue, plane, rows):
+def load_scale_rows(queues, plane, rows, copies):
     words = rows.bitcast(I32)
     width = words.shape[1]
     for q in range(4):
-        quad = words[4 * q : 4 * q + 4, :].unsqueeze(0).to_broadcast([8, 4, width])
-        queue.dma_start(out=plane[32 * q : 32 * q + 32, :].bitcast(I32), in_=quad)
+        quad = words[4 * q : 4 * q + 4, :]
+        queues[q].dma_start(out=plane[32 * q : 32 * q + 4 * copies, :].bitcast(I32), in_=quad)
 
 
 def tile_list_hwayt_hl_gelu_kernel(
@@ -50,55 +50,66 @@ def tile_list_hwayt_hl_gelu_kernel(
         w_raw = [sb.tile([P, PACK, P], F32, name="w_raw%d" % u, align_bytes=64) for u in range(TILES)]
         r_rows = [sb.tile([P, T], F32, name="r_rows%d" % u, align_bytes=64) for u in range(TILES)]
 
+        nc.vector.memset(tab_plane[:].bitcast(I32), 0)
+        nc.vector.memset(wg_plane[:].bitcast(I32), 0)
         nc.gpsimd.memset(warm[:], 0.0)
         nc.scalar.activation(warm_out[:], warm[:], ACT.Gelu_apprx_tanh)
-
         nc.sync.dma_start(offsets[:], offs)
-        load_scale_rows(nc.sync, tab_plane, tab_scales[0])
-        nc.sync.dma_start(out=tab_codes[:].bitcast(I32), in_=tab_words[0].rearrange("p t i -> p (t i)").bitcast(I32))
-        wh_rows = wh.rearrange("(p i) n -> p i n", i=PACK)
-        for u in range(TILES):
-            nc.sync.dma_start(out=w_raw[u][:], in_=wh_rows[:, :, u * P : (u + 1) * P])
         nc.sync.dma_start(out=wg_codes[:].bitcast(I32), in_=wg_words[0].bitcast(I32))
-        load_scale_rows(nc.sync, wg_plane, wg_scales[0])
+        load_scale_rows([nc.sync, nc.sync, nc.sync, nc.sync], tab_plane, tab_scales[0], 1)
+        nc.sync.dma_start(out=tab_codes[:].bitcast(I32), in_=tab_words[0].rearrange("p t i -> p (t i)").bitcast(I32))
+        nc.sync.dma_start(out=w_raw[0][:], in_=wh.rearrange("(p i) n -> p i n", i=PACK)[:, :, 0 * P : (0 + 1) * P])
+        nc.sync.dma_start(out=w_raw[1][:], in_=wh.rearrange("(p i) n -> p i n", i=PACK)[:, :, 1 * P : (1 + 1) * P])
+        load_scale_rows([nc.sync, nc.sync, nc.sync, nc.sync], wg_plane, wg_scales[0], 1)
         with nc.allow_non_contiguous_dma(reason="one bias value a partition"):
             nc.sync.dma_start(out=bias[:], in_=bg.rearrange("(u p) -> p u", p=P))
-        for u in range(TILES):
-            nc.sync.dma_start(out=r_rows[u][:], in_=rT[u * P : (u + 1) * P, :])
+        nc.sync.dma_start(out=r_rows[0][:], in_=rT[0 * P : (0 + 1) * P, :])
+        nc.sync.dma_start(out=r_rows[1][:], in_=rT[1 * P : (1 + 1) * P, :])
 
         v_plane = sb.tile([P, J], U8, name="v_plane", align_bytes=64)
         v_codes = sb.tile([P, J], U32, name="v_codes", align_bytes=64)
         nc.vector.tensor_copy(v_plane[:], tab_plane[:].indirect(offsets[:]))
         nc.vector.tensor_copy(v_codes[:], tab_codes[:].indirect(offsets[:]))
 
-        nc.scalar.mul(half_bias[:], bias[:], 0.5)
+        def tiles(name, shape, dtype):
+            return [sb.tile(shape, dtype, name="%s%d" % (name, u), align_bytes=64) for u in range(TILES)]
 
-        w_codes, w_plane = [], []
-        for u in range(TILES):
-            upper = sb.tile([P, P, PACK], BF16, name="upper%d" % u, align_bytes=64)
-            parts = sb.tile([P, 2 * P * PACK], BF16, name="parts%d" % u, align_bytes=64)
-            codes = sb.tile([P, 2 * P], U32, name="w_codes%d" % u, align_bytes=64)
-            plane = sb.tile([P, 2 * P], U8, name="w_plane%d" % u, align_bytes=64)
+        upper = tiles("upper", [P, P, PACK], BF16)
+        parts = tiles("parts", [P, 2 * P * PACK], BF16)
+        w_codes = tiles("w_codes", [P, 2 * P], U32)
+        w_plane = tiles("w_plane", [P, 2 * P], U8)
+        tanhs = tiles("tanh", [P, J], F32)
+        keeps = tiles("keep", [P, J], F32)
+        gelus = tiles("gelu", [P, J], F32)
+        carried = tiles("carried", [P, J], F32)
+        made = tiles("made", [P, J], F32)
+        result = tiles("result", [P, J], F32)
+
+        def take_upper(u):
             halves = w_raw[u][:].bitcast(BF16).rearrange("p i (n h) -> p n i h", h=2)
-            nc.scalar.copy(upper[:], halves[:, :, :, 1])
-            hi = parts[:, 0 : P * PACK]
-            lo = parts[:, P * PACK : 2 * P * PACK]
+            nc.scalar.copy(upper[u][:], halves[:, :, :, 1])
+
+        def cut_hi(u):
+            hi = parts[u][:, 0 : P * PACK]
             nc.vector.tensor_single_scalar(
-                hi.bitcast(I32), upper[:].rearrange("p n i -> p (n i)").bitcast(I32), HI_MASK_PAIR, ALU.bitwise_and
+                hi.bitcast(I32), upper[u][:].rearrange("p n i -> p (n i)").bitcast(I32), HI_MASK_PAIR, ALU.bitwise_and
             )
+
+        def cut_lo(u):
+            hi = parts[u][:, 0 : P * PACK]
+            lo = parts[u][:, P * PACK : 2 * P * PACK]
             nc.vector.tensor_tensor(
                 lo.rearrange("p (n i) -> p n i", i=PACK),
                 w_raw[u][:].rearrange("p i n -> p n i"),
                 hi.rearrange("p (n i) -> p n i", i=PACK),
                 ALU.subtract,
             )
-            nc.vector.quantize_mx(out=codes[:].bitcast(FP8X4), scales=plane[:], in_=parts[:])
-            w_codes.append(codes)
-            w_plane.append(plane)
 
-        tanhs, gelus = [], []
-        for u in range(TILES):
-            ga = ps.tile([P, J], F32, name="ga%d" % u)
+        def quantise(u):
+            nc.vector.quantize_mx(out=w_codes[u][:].bitcast(FP8X4), scales=w_plane[u][:], in_=parts[u][:])
+
+        def gate(u):
+            ga = ps.tile([P, J], F32, name="bank%d" % u)
             nc.tensor.matmul_mx(
                 out=ga[:],
                 lhsT=wg_codes[:, 2 * u * P : 2 * (u + 1) * P].bitcast(FP4X4),
@@ -108,11 +119,11 @@ def tile_list_hwayt_hl_gelu_kernel(
                 start=True,
                 stop=True,
             )
-            th = sb.tile([P, J], F32, name="tanh%d" % u, align_bytes=64)
-            nc.scalar.activation(th[:], ga[:], ACT.Tanh, bias=half_bias[:, u : u + 1], scale=0.5)
-            tanhs.append(th)
-        for u in range(TILES):
-            ha = ps.tile([P, J], F32, name="ha%d" % u)
+            nc.scalar.activation(tanhs[u][:], ga[:], ACT.Tanh, bias=half_bias[:, u : u + 1], scale=0.5)
+            nc.scalar.activation(keeps[u][:], tanhs[u][:], ACT.Identity, bias=0.5, scale=-0.5)
+
+        def transform(u):
+            ha = ps.tile([P, J], F32, name="bank%d" % u)
             for part in range(2):
                 cols = slice(part * P, (part + 1) * P)
                 nc.tensor.matmul_mx(
@@ -124,20 +135,35 @@ def tile_list_hwayt_hl_gelu_kernel(
                     start=(part == 0),
                     stop=(part == 1),
                 )
-            h = sb.tile([P, J], F32, name="gelu%d" % u, align_bytes=64)
-            nc.scalar.activation(h[:], ha[:], ACT.Gelu_apprx_tanh)
-            gelus.append(h)
+            nc.scalar.activation(gelus[u][:], ha[:], ACT.Gelu_apprx_tanh)
 
-        diffs, scaled = [], []
-        for u in range(TILES):
-            d = sb.tile([P, J], F32, name="diff%d" % u, align_bytes=64)
-            nc.vector.tensor_tensor(d[:], r_rows[u][:].indirect(offsets[:]), gelus[u][:], ALU.subtract)
-            diffs.append(d)
-        for u in range(TILES):
-            e = sb.tile([P, J], F32, name="scaled%d" % u, align_bytes=64)
-            nc.vector.scalar_tensor_tensor(e[:], tanhs[u][:], 1.0, diffs[u][:], ALU.subtract, ALU.mult)
-            scaled.append(e)
-        for u in range(TILES):
-            o = sb.tile([P, J], F32, name="result%d" % u, align_bytes=64)
-            nc.vector.scalar_tensor_tensor(o[:], scaled[u][:], -0.5, gelus[u][:], ALU.mult, ALU.add)
-            nc.sync.dma_start(out=out[u * P : (u + 1) * P, :], in_=o[:])
+        def carry(u):
+            nc.vector.tensor_tensor(carried[u][:], r_rows[u][:].indirect(offsets[:]), keeps[u][:], ALU.mult)
+
+        def make(u):
+            nc.vector.scalar_tensor_tensor(made[u][:], tanhs[u][:], 1.0, gelus[u][:], ALU.add, ALU.mult)
+
+        def finish(u, cols):
+            nc.vector.scalar_tensor_tensor(result[u][:, cols], made[u][:, cols], 0.5, carried[u][:, cols], ALU.mult, ALU.add)
+            nc.sync.dma_start(out=out[u * P : (u + 1) * P, cols], in_=result[u][:, cols])
+
+        take_upper(0)
+        take_upper(1)
+        nc.scalar.mul(half_bias[:], bias[:], 0.5)
+        cut_hi(0)
+        cut_lo(0)
+        cut_hi(1)
+        quantise(0)
+        cut_lo(1)
+        gate(0)
+        gate(1)
+        transform(0)
+        carry(0)
+        quantise(1)
+        transform(1)
+        carry(1)
+        make(0)
+        make(1)
+        finish(0, slice(0, J))
+        finish(1, slice(0, J // 2))
+        finish(1, slice(J // 2, J))

@@ -19,15 +19,15 @@ ACT = mybir.ActivationFunctionType
 P = 128
 PACK = 4
 TILES = N // P
-HI_MASK_PAIR = 0xFFF0FFF0 - (1 << 32)
+HI_MASK = 0xFFF00000 - (1 << 32)
+HALF = J // 2
+SPLIT = 192
 
 
-def load_scale_rows(queues, plane, rows, copies):
+def load_scale_rows(nc, plane, rows):
     words = rows.bitcast(I32)
-    width = words.shape[1]
     for q in range(4):
-        quad = words[4 * q : 4 * q + 4, :]
-        queues[q].dma_start(out=plane[32 * q : 32 * q + 4 * copies, :].bitcast(I32), in_=quad)
+        nc.sync.dma_start(out=plane[32 * q : 32 * q + 4, :].bitcast(I32), in_=words[4 * q : 4 * q + 4, :])
 
 
 def tile_list_hwayt_hl_gelu_kernel(
@@ -47,89 +47,102 @@ def tile_list_hwayt_hl_gelu_kernel(
         half_bias = sb.tile([P, TILES], F32, name="half_bias")
         warm = sb.tile([P, 1], F32, name="warm")
         warm_out = sb.tile([P, 1], F32, name="warm_out")
-        w_raw = [sb.tile([P, PACK, P], F32, name="w_raw%d" % u, align_bytes=64) for u in range(TILES)]
+        w_raw = sb.tile([P, PACK, N], F32, name="w_raw", align_bytes=64)
         r_rows = [sb.tile([P, T], F32, name="r_rows%d" % u, align_bytes=64) for u in range(TILES)]
 
         nc.vector.memset(tab_plane[:].bitcast(I32), 0)
         nc.vector.memset(wg_plane[:].bitcast(I32), 0)
         nc.gpsimd.memset(warm[:], 0.0)
         nc.scalar.activation(warm_out[:], warm[:], ACT.Gelu_apprx_tanh)
+        nc.sync.dma_start(out=w_raw[:], in_=wh.rearrange("(p i) n -> p i n", i=PACK))
         nc.sync.dma_start(offsets[:], offs)
-        nc.sync.dma_start(out=wg_codes[:].bitcast(I32), in_=wg_words[0].bitcast(I32))
-        load_scale_rows([nc.sync, nc.sync, nc.sync, nc.sync], tab_plane, tab_scales[0], 1)
+        load_scale_rows(nc, tab_plane, tab_scales[0])
         nc.sync.dma_start(out=tab_codes[:].bitcast(I32), in_=tab_words[0].rearrange("p t i -> p (t i)").bitcast(I32))
-        nc.sync.dma_start(out=w_raw[0][:], in_=wh.rearrange("(p i) n -> p i n", i=PACK)[:, :, 0 * P : (0 + 1) * P])
-        nc.sync.dma_start(out=w_raw[1][:], in_=wh.rearrange("(p i) n -> p i n", i=PACK)[:, :, 1 * P : (1 + 1) * P])
-        load_scale_rows([nc.sync, nc.sync, nc.sync, nc.sync], wg_plane, wg_scales[0], 1)
+        nc.sync.dma_start(out=wg_codes[:].bitcast(I32), in_=wg_words[0].bitcast(I32))
+        load_scale_rows(nc, wg_plane, wg_scales[0])
         with nc.allow_non_contiguous_dma(reason="one bias value a partition"):
             nc.sync.dma_start(out=bias[:], in_=bg.rearrange("(u p) -> p u", p=P))
-        nc.sync.dma_start(out=r_rows[0][:], in_=rT[0 * P : (0 + 1) * P, :])
-        nc.sync.dma_start(out=r_rows[1][:], in_=rT[1 * P : (1 + 1) * P, :])
-
-        v_plane = sb.tile([P, J], U8, name="v_plane", align_bytes=64)
-        v_codes = sb.tile([P, J], U32, name="v_codes", align_bytes=64)
-        nc.vector.tensor_copy(v_plane[:], tab_plane[:].indirect(offsets[:]))
-        nc.vector.tensor_copy(v_codes[:], tab_codes[:].indirect(offsets[:]))
+        nc.sync.dma_start(out=r_rows[1][:], in_=rT[P : 2 * P, :])
+        nc.sync.dma_start(out=r_rows[0][:], in_=rT[0:P, :])
 
         def tiles(name, shape, dtype):
             return [sb.tile(shape, dtype, name="%s%d" % (name, u), align_bytes=64) for u in range(TILES)]
 
-        upper = tiles("upper", [P, P, PACK], BF16)
-        parts = tiles("parts", [P, 2 * P * PACK], BF16)
+        width = P * PACK
+        parts = sb.tile([P, 4 * width], BF16, name="parts", align_bytes=64)
+        his = [parts[:, 0:width], parts[:, 3 * width : 4 * width]]
+        lo = parts[:, width : 3 * width].rearrange("p (n i) -> p n i", i=PACK)
+        hi32 = sb.tile([P, N, PACK], F32, name="hi32", align_bytes=64)
         w_codes = tiles("w_codes", [P, 2 * P], U32)
         w_plane = tiles("w_plane", [P, 2 * P], U8)
-        tanhs = tiles("tanh", [P, J], F32)
-        keeps = tiles("keep", [P, J], F32)
+        tanh1 = sb.tile([P, J], F32, name="tanh1", align_bytes=64)
         gelus = tiles("gelu", [P, J], F32)
-        carried = tiles("carried", [P, J], F32)
-        made = tiles("made", [P, J], F32)
         result = tiles("result", [P, J], F32)
+        keep = sb.tile([P, J], F32, name="keep", align_bytes=64)
+        made = sb.tile([P, J], F32, name="made", align_bytes=64)
+        diff = sb.tile([P, J], F32, name="diff", align_bytes=64)
+        scaled = sb.tile([P, J], F32, name="scaled", align_bytes=64)
+        carried = parts[:, 0 : 2 * width].bitcast(F32)
+        v_plane = sb.tile([P, J], U8, name="v_plane", align_bytes=64)
+        v_codes = sb.tile([P, J], U32, name="v_codes", align_bytes=64)
+        woven = w_raw[:].rearrange("p i n -> p n i")
+        woven_bits = w_raw[:].bitcast(I32).rearrange("p i n -> p n i")
+        spans = [slice(0, HALF), slice(HALF, J)]
+        whole = slice(0, J)
 
-        def take_upper(u):
-            halves = w_raw[u][:].bitcast(BF16).rearrange("p i (n h) -> p n i h", h=2)
-            nc.scalar.copy(upper[u][:], halves[:, :, :, 1])
+        def listed(cols):
+            return offsets[:, cols.start // 16 : cols.stop // 16]
 
-        def cut_hi(u):
-            hi = parts[u][:, 0 : P * PACK]
+        def cut_hi(chans):
             nc.vector.tensor_single_scalar(
-                hi.bitcast(I32), upper[u][:].rearrange("p n i -> p (n i)").bitcast(I32), HI_MASK_PAIR, ALU.bitwise_and
+                hi32[:].bitcast(I32)[:, chans, :], woven_bits[:, chans, :], HI_MASK, ALU.bitwise_and
             )
 
-        def cut_lo(u):
-            hi = parts[u][:, 0 : P * PACK]
-            lo = parts[u][:, P * PACK : 2 * P * PACK]
-            nc.vector.tensor_tensor(
-                lo.rearrange("p (n i) -> p n i", i=PACK),
-                w_raw[u][:].rearrange("p i n -> p n i"),
-                hi.rearrange("p (n i) -> p n i", i=PACK),
-                ALU.subtract,
-            )
+        def cut_lo(engine, chans):
+            engine.tensor_tensor(lo[:, chans, :], woven[:, chans, :], hi32[:, chans, :], ALU.subtract)
 
         def quantise(u):
-            nc.vector.quantize_mx(out=w_codes[u][:].bitcast(FP8X4), scales=w_plane[u][:], in_=parts[u][:])
+            nc.vector.quantize_mx(
+                out=w_codes[u][:].bitcast(FP8X4),
+                scales=w_plane[u][:],
+                in_=parts[:, 2 * u * width : 2 * (u + 1) * width],
+            )
 
-        def gate(u):
-            ga = ps.tile([P, J], F32, name="bank%d" % u)
+        cut_hi(slice(SPLIT, N))
+        cut_hi(slice(0, SPLIT))
+        cut_lo(nc.vector, slice(SPLIT, N))
+        cut_lo(nc.gpsimd, slice(0, SPLIT))
+        for u in range(TILES):
+            nc.scalar.copy(his[u], hi32[:, u * P : (u + 1) * P, :].rearrange("p n i -> p (n i)"))
+        nc.scalar.mul(half_bias[:], bias[:], 0.5)
+        nc.vector.tensor_copy(v_plane[:], tab_plane[:].indirect(offsets[:]))
+        for cols in spans:
+            nc.vector.tensor_copy(v_codes[:, cols], tab_codes[:].indirect(listed(cols)))
+
+        def gate_sum(u, cols, bank):
+            ga = ps.tile([P, cols.stop - cols.start], F32, name=bank)
             nc.tensor.matmul_mx(
                 out=ga[:],
                 lhsT=wg_codes[:, 2 * u * P : 2 * (u + 1) * P].bitcast(FP4X4),
                 lhsT_scale=wg_plane[:, u * P : (u + 1) * P],
-                rhs=v_codes[:].bitcast(FP8X4),
-                rhs_scale=v_plane[:],
+                rhs=v_codes[:, cols].bitcast(FP8X4),
+                rhs_scale=v_plane[:, cols],
                 start=True,
                 stop=True,
             )
-            nc.scalar.activation(tanhs[u][:], ga[:], ACT.Tanh, bias=half_bias[:, u : u + 1], scale=0.5)
-            nc.scalar.activation(keeps[u][:], tanhs[u][:], ACT.Identity, bias=0.5, scale=-0.5)
+            return ga
 
-        def transform(u):
-            ha = ps.tile([P, J], F32, name="bank%d" % u)
+        def gate_tanh(u, ga, dest):
+            nc.scalar.activation(dest, ga[:], ACT.Tanh, bias=half_bias[:, u : u + 1], scale=0.5)
+
+        def transform(u, bank):
+            ha = ps.tile([P, J], F32, name=bank)
             for part in range(2):
-                cols = slice(part * P, (part + 1) * P)
+                chans = slice(part * P, (part + 1) * P)
                 nc.tensor.matmul_mx(
                     out=ha[:],
-                    lhsT=w_codes[u][:, cols].bitcast(FP8X4),
-                    lhsT_scale=w_plane[u][:, cols],
+                    lhsT=w_codes[u][:, chans].bitcast(FP8X4),
+                    lhsT_scale=w_plane[u][:, chans],
                     rhs=v_codes[:].bitcast(FP8X4),
                     rhs_scale=v_plane[:],
                     start=(part == 0),
@@ -137,33 +150,22 @@ def tile_list_hwayt_hl_gelu_kernel(
                 )
             nc.scalar.activation(gelus[u][:], ha[:], ACT.Gelu_apprx_tanh)
 
-        def carry(u):
-            nc.vector.tensor_tensor(carried[u][:], r_rows[u][:].indirect(offsets[:]), keeps[u][:], ALU.mult)
-
-        def make(u):
-            nc.vector.scalar_tensor_tensor(made[u][:], tanhs[u][:], 1.0, gelus[u][:], ALU.add, ALU.mult)
-
-        def finish(u, cols):
-            nc.vector.scalar_tensor_tensor(result[u][:, cols], made[u][:, cols], 0.5, carried[u][:, cols], ALU.mult, ALU.add)
-            nc.sync.dma_start(out=out[u * P : (u + 1) * P, cols], in_=result[u][:, cols])
-
-        take_upper(0)
-        take_upper(1)
-        nc.scalar.mul(half_bias[:], bias[:], 0.5)
-        cut_hi(0)
-        cut_lo(0)
-        cut_hi(1)
+        for half, cols in enumerate(spans):
+            gate_tanh(1, gate_sum(1, cols, "bank%d" % half), tanh1[:, cols])
+            nc.scalar.activation(keep[:, cols], tanh1[:, cols], ACT.Identity, bias=0.5, scale=-0.5)
         quantise(0)
-        cut_lo(1)
-        gate(0)
-        gate(1)
-        transform(0)
-        carry(0)
         quantise(1)
-        transform(1)
-        carry(1)
-        make(0)
-        make(1)
-        finish(0, slice(0, J))
-        finish(1, slice(0, J // 2))
-        finish(1, slice(J // 2, J))
+        late_sum = gate_sum(0, whole, "bank2")
+        transform(0, "bank0")
+        transform(1, "bank1")
+        for cols in spans:
+            nc.vector.tensor_tensor(carried[:, cols], r_rows[1][:].indirect(listed(cols)), keep[:, cols], ALU.mult)
+        gate_tanh(0, late_sum, keep[:])
+        nc.vector.tensor_tensor(diff[:], r_rows[0][:].indirect(offsets[:]), gelus[0][:], ALU.subtract)
+        nc.vector.scalar_tensor_tensor(made[:], tanh1[:], 1.0, gelus[1][:], ALU.add, ALU.mult)
+        nc.vector.scalar_tensor_tensor(scaled[:], keep[:], 1.0, diff[:], ALU.subtract, ALU.mult)
+        nc.vector.scalar_tensor_tensor(result[1][:], made[:], 0.5, carried, ALU.mult, ALU.add)
+        nc.sync.dma_start(out=out[P : 2 * P, :], in_=result[1][:])
+        for cols in spans:
+            nc.vector.scalar_tensor_tensor(result[0][:, cols], scaled[:, cols], -0.5, gelus[0][:, cols], ALU.mult, ALU.add)
+            nc.sync.dma_start(out=out[0:P, cols], in_=result[0][:, cols])

@@ -21,7 +21,8 @@ PACK = 4
 TILES = N // P
 HI_MASK = 0xFFF00000 - (1 << 32)
 HALF = J // 2
-SPLIT = 192
+LONG = 320
+HI_MASK_PAIR = 0xFFF0FFF0 - (1 << 32)
 
 
 def load_scale_rows(nc, plane, rows):
@@ -47,17 +48,19 @@ def tile_list_hwayt_hl_gelu_kernel(
         half_bias = sb.tile([P, TILES], F32, name="half_bias")
         warm = sb.tile([P, 1], F32, name="warm")
         warm_out = sb.tile([P, 1], F32, name="warm_out")
-        w_raw = sb.tile([P, PACK, N], F32, name="w_raw", align_bytes=64)
+        w_raw = [sb.tile([P, PACK, P], F32, name="w_raw%d" % u, align_bytes=64) for u in range(TILES)]
         r_rows = [sb.tile([P, T], F32, name="r_rows%d" % u, align_bytes=64) for u in range(TILES)]
 
         nc.vector.memset(tab_plane[:].bitcast(I32), 0)
         nc.vector.memset(wg_plane[:].bitcast(I32), 0)
         nc.gpsimd.memset(warm[:], 0.0)
         nc.scalar.activation(warm_out[:], warm[:], ACT.Gelu_apprx_tanh)
-        nc.sync.dma_start(out=w_raw[:], in_=wh.rearrange("(p i) n -> p i n", i=PACK))
+        w_rows = wh.rearrange("(p i) n -> p i n", i=PACK)
+        nc.sync.dma_start(out=w_raw[0][:], in_=w_rows[:, :, 0:P])
         nc.sync.dma_start(offsets[:], offs)
         load_scale_rows(nc, tab_plane, tab_scales[0])
         nc.sync.dma_start(out=tab_codes[:].bitcast(I32), in_=tab_words[0].rearrange("p t i -> p (t i)").bitcast(I32))
+        nc.sync.dma_start(out=w_raw[1][:], in_=w_rows[:, :, P : 2 * P])
         nc.sync.dma_start(out=wg_codes[:].bitcast(I32), in_=wg_words[0].bitcast(I32))
         load_scale_rows(nc, wg_plane, wg_scales[0])
         with nc.allow_non_contiguous_dma(reason="one bias value a partition"):
@@ -69,10 +72,9 @@ def tile_list_hwayt_hl_gelu_kernel(
             return [sb.tile(shape, dtype, name="%s%d" % (name, u), align_bytes=64) for u in range(TILES)]
 
         width = P * PACK
-        parts = sb.tile([P, 4 * width], BF16, name="parts", align_bytes=64)
-        his = [parts[:, 0:width], parts[:, 3 * width : 4 * width]]
-        lo = parts[:, width : 3 * width].rearrange("p (n i) -> p n i", i=PACK)
-        hi32 = sb.tile([P, N, PACK], F32, name="hi32", align_bytes=64)
+        hi32 = sb.tile([P, P, PACK], F32, name="hi32", align_bytes=64)
+        upper = sb.tile([P, P, PACK], BF16, name="upper", align_bytes=64)
+        parts0 = sb.tile([P, 2 * width], BF16, name="parts0", align_bytes=64)
         w_codes = tiles("w_codes", [P, 2 * P], U32)
         w_plane = tiles("w_plane", [P, 2 * P], U8)
         tanh1 = sb.tile([P, J], F32, name="tanh1", align_bytes=64)
@@ -82,42 +84,40 @@ def tile_list_hwayt_hl_gelu_kernel(
         made = sb.tile([P, J], F32, name="made", align_bytes=64)
         diff = sb.tile([P, J], F32, name="diff", align_bytes=64)
         scaled = sb.tile([P, J], F32, name="scaled", align_bytes=64)
-        carried = parts[:, 0 : 2 * width].bitcast(F32)
+        carried = parts0[:].bitcast(F32)
         v_plane = sb.tile([P, J], U8, name="v_plane", align_bytes=64)
         v_codes = sb.tile([P, J], U32, name="v_codes", align_bytes=64)
-        woven = w_raw[:].rearrange("p i n -> p n i")
-        woven_bits = w_raw[:].bitcast(I32).rearrange("p i n -> p n i")
+        woven = [w_raw[u][:].rearrange("p i n -> p n i") for u in range(TILES)]
         spans = [slice(0, HALF), slice(HALF, J)]
         whole = slice(0, J)
 
         def listed(cols):
             return offsets[:, cols.start // 16 : cols.stop // 16]
 
-        def cut_hi(chans):
-            nc.vector.tensor_single_scalar(
-                hi32[:].bitcast(I32)[:, chans, :], woven_bits[:, chans, :], HI_MASK, ALU.bitwise_and
-            )
+        def by_word(ap):
+            return ap.rearrange("p (n i) -> p n i", i=PACK)
 
-        def cut_lo(engine, chans):
-            engine.tensor_tensor(lo[:, chans, :], woven[:, chans, :], hi32[:, chans, :], ALU.subtract)
+        def quantise(u, parts):
+            nc.vector.quantize_mx(out=w_codes[u][:].bitcast(FP8X4), scales=w_plane[u][:], in_=parts[:])
 
-        def quantise(u):
-            nc.vector.quantize_mx(
-                out=w_codes[u][:].bitcast(FP8X4),
-                scales=w_plane[u][:],
-                in_=parts[:, 2 * u * width : 2 * (u + 1) * width],
-            )
-
-        cut_hi(slice(SPLIT, N))
-        cut_hi(slice(0, SPLIT))
-        cut_lo(nc.vector, slice(SPLIT, N))
-        cut_lo(nc.gpsimd, slice(0, SPLIT))
-        for u in range(TILES):
-            nc.scalar.copy(his[u], hi32[:, u * P : (u + 1) * P, :].rearrange("p n i -> p (n i)"))
+        nc.vector.tensor_single_scalar(
+            hi32[:].bitcast(I32), w_raw[0][:].bitcast(I32).rearrange("p i n -> p n i"), HI_MASK, ALU.bitwise_and
+        )
+        nc.gpsimd.tensor_tensor(by_word(parts0[:, width : 2 * width]), woven[0], hi32[:], ALU.subtract)
+        halves = w_raw[1][:].bitcast(BF16).rearrange("p i (n h) -> p n i h", h=2)
+        nc.scalar.copy(parts0[:, 0:width], hi32[:].rearrange("p n i -> p (n i)"))
+        nc.scalar.copy(upper[:], halves[:, :, :, 1])
         nc.scalar.mul(half_bias[:], bias[:], 0.5)
         nc.vector.tensor_copy(v_plane[:], tab_plane[:].indirect(offsets[:]))
         for cols in spans:
             nc.vector.tensor_copy(v_codes[:, cols], tab_codes[:].indirect(listed(cols)))
+        parts1 = sb.tile([P, 2 * width], BF16, name="parts1", align_bytes=64)
+        nc.vector.tensor_single_scalar(
+            parts1[:, 0:width].bitcast(I32),
+            upper[:].rearrange("p n i -> p (n i)").bitcast(I32),
+            HI_MASK_PAIR,
+            ALU.bitwise_and,
+        )
 
         def gate_sum(u, cols, bank):
             ga = ps.tile([P, cols.stop - cols.start], F32, name=bank)
@@ -133,7 +133,7 @@ def tile_list_hwayt_hl_gelu_kernel(
             return ga
 
         def gate_tanh(u, ga, dest):
-            nc.scalar.activation(dest, ga[:], ACT.Tanh, bias=half_bias[:, u : u + 1], scale=0.5)
+            nc.scalar.activation(dest, ga, ACT.Tanh, bias=half_bias[:, u : u + 1], scale=0.5)
 
         def transform(u, bank):
             ha = ps.tile([P, J], F32, name=bank)
@@ -151,21 +151,31 @@ def tile_list_hwayt_hl_gelu_kernel(
             nc.scalar.activation(gelus[u][:], ha[:], ACT.Gelu_apprx_tanh)
 
         for half, cols in enumerate(spans):
-            gate_tanh(1, gate_sum(1, cols, "bank%d" % half), tanh1[:, cols])
+            gate_tanh(1, gate_sum(1, cols, "bank%d" % half)[:], tanh1[:, cols])
             nc.scalar.activation(keep[:, cols], tanh1[:, cols], ACT.Identity, bias=0.5, scale=-0.5)
-        quantise(0)
-        quantise(1)
         late_sum = gate_sum(0, whole, "bank2")
+        quantise(0, parts0)
         transform(0, "bank0")
+        nc.vector.tensor_tensor(
+            by_word(parts1[:, width : 2 * width]), woven[1], by_word(parts1[:, 0:width]), ALU.subtract
+        )
+        quantise(1, parts1)
         transform(1, "bank1")
+        nc.vector.tensor_tensor(carried[:, spans[0]], r_rows[1][:].indirect(listed(spans[0])), keep[:, spans[0]], ALU.mult)
+        nc.vector.tensor_tensor(carried[:, spans[1]], r_rows[1][:].indirect(listed(spans[1])), keep[:, spans[1]], ALU.mult)
         for cols in spans:
-            nc.vector.tensor_tensor(carried[:, cols], r_rows[1][:].indirect(listed(cols)), keep[:, cols], ALU.mult)
-        gate_tanh(0, late_sum, keep[:])
+            gate_tanh(0, late_sum[:, cols], keep[:, cols])
         nc.vector.tensor_tensor(diff[:], r_rows[0][:].indirect(offsets[:]), gelus[0][:], ALU.subtract)
         nc.vector.scalar_tensor_tensor(made[:], tanh1[:], 1.0, gelus[1][:], ALU.add, ALU.mult)
-        nc.vector.scalar_tensor_tensor(scaled[:], keep[:], 1.0, diff[:], ALU.subtract, ALU.mult)
+        ends = [slice(0, LONG), slice(LONG, J)]
+
+        def scale(cols):
+            nc.vector.scalar_tensor_tensor(scaled[:, cols], keep[:, cols], 1.0, diff[:, cols], ALU.subtract, ALU.mult)
+
+        scale(ends[0])
         nc.vector.scalar_tensor_tensor(result[1][:], made[:], 0.5, carried, ALU.mult, ALU.add)
         nc.sync.dma_start(out=out[P : 2 * P, :], in_=result[1][:])
-        for cols in spans:
+        scale(ends[1])
+        for cols in ends:
             nc.vector.scalar_tensor_tensor(result[0][:, cols], scaled[:, cols], -0.5, gelus[0][:, cols], ALU.mult, ALU.add)
             nc.sync.dma_start(out=out[0:P, cols], in_=result[0][:, cols])

@@ -25,10 +25,10 @@ LONG = 320
 HI_MASK_PAIR = 0xFFF0FFF0 - (1 << 32)
 
 
-def load_scale_rows(nc, plane, rows):
+def load_scale_rows(queues, plane, rows):
     words = rows.bitcast(I32)
     for q in range(4):
-        nc.sync.dma_start(out=plane[32 * q : 32 * q + 4, :].bitcast(I32), in_=words[4 * q : 4 * q + 4, :])
+        queues[q].dma_start(out=plane[32 * q : 32 * q + 4, :].bitcast(I32), in_=words[4 * q : 4 * q + 4, :])
 
 
 def tile_list_hwayt_hl_gelu_kernel(
@@ -53,16 +53,16 @@ def tile_list_hwayt_hl_gelu_kernel(
 
         nc.vector.memset(tab_plane[:].bitcast(I32), 0)
         nc.vector.memset(wg_plane[:].bitcast(I32), 0)
-        nc.gpsimd.memset(warm[:], 0.0)
-        nc.scalar.activation(warm_out[:], warm[:], ACT.Gelu_apprx_tanh)
+        nc.vector.memset(warm[:], 0.0)
         w_rows = wh.rearrange("(p i) n -> p i n", i=PACK)
         nc.sync.dma_start(out=w_raw[0][:], in_=w_rows[:, :, 0:P])
         nc.sync.dma_start(offsets[:], offs)
-        load_scale_rows(nc, tab_plane, tab_scales[0])
+        load_scale_rows([nc.sync, nc.scalar, nc.sync, nc.scalar], tab_plane, tab_scales[0])
+        nc.scalar.activation(warm_out[:], warm[:], ACT.Gelu_apprx_tanh)
         nc.sync.dma_start(out=tab_codes[:].bitcast(I32), in_=tab_words[0].rearrange("p t i -> p (t i)").bitcast(I32))
         nc.sync.dma_start(out=w_raw[1][:], in_=w_rows[:, :, P : 2 * P])
         nc.sync.dma_start(out=wg_codes[:].bitcast(I32), in_=wg_words[0].bitcast(I32))
-        load_scale_rows(nc, wg_plane, wg_scales[0])
+        load_scale_rows([nc.sync] * 4, wg_plane, wg_scales[0])
         with nc.allow_non_contiguous_dma(reason="one bias value a partition"):
             nc.sync.dma_start(out=bias[:], in_=bg.rearrange("(u p) -> p u", p=P))
         nc.sync.dma_start(out=r_rows[1][:], in_=rT[P : 2 * P, :])
@@ -74,7 +74,9 @@ def tile_list_hwayt_hl_gelu_kernel(
         width = P * PACK
         hi32 = sb.tile([P, P, PACK], F32, name="hi32", align_bytes=64)
         upper = sb.tile([P, P, PACK], BF16, name="upper", align_bytes=64)
-        parts0 = sb.tile([P, 2 * width], BF16, name="parts0", align_bytes=64)
+        parts = sb.tile([P, 3 * width], BF16, name="parts", align_bytes=64)
+        parts0 = parts[:, 0 : 2 * width]
+        parts1 = parts[:, width : 3 * width]
         w_codes = tiles("w_codes", [P, 2 * P], U32)
         w_plane = tiles("w_plane", [P, 2 * P], U8)
         tanh1 = sb.tile([P, J], F32, name="tanh1", align_bytes=64)
@@ -84,7 +86,7 @@ def tile_list_hwayt_hl_gelu_kernel(
         made = sb.tile([P, J], F32, name="made", align_bytes=64)
         diff = sb.tile([P, J], F32, name="diff", align_bytes=64)
         scaled = sb.tile([P, J], F32, name="scaled", align_bytes=64)
-        carried = parts0[:].bitcast(F32)
+        carried = sb.tile([P, J], F32, name="carried", align_bytes=64)
         v_plane = sb.tile([P, J], U8, name="v_plane", align_bytes=64)
         v_codes = sb.tile([P, J], U32, name="v_codes", align_bytes=64)
         woven = [w_raw[u][:].rearrange("p i n -> p n i") for u in range(TILES)]
@@ -97,8 +99,8 @@ def tile_list_hwayt_hl_gelu_kernel(
         def by_word(ap):
             return ap.rearrange("p (n i) -> p n i", i=PACK)
 
-        def quantise(u, parts):
-            nc.vector.quantize_mx(out=w_codes[u][:].bitcast(FP8X4), scales=w_plane[u][:], in_=parts[:])
+        def quantise(u, staged):
+            nc.vector.quantize_mx(out=w_codes[u][:].bitcast(FP8X4), scales=w_plane[u][:], in_=staged)
 
         nc.vector.tensor_single_scalar(
             hi32[:].bitcast(I32), w_raw[0][:].bitcast(I32).rearrange("p i n -> p n i"), HI_MASK, ALU.bitwise_and
@@ -111,18 +113,16 @@ def tile_list_hwayt_hl_gelu_kernel(
         nc.vector.tensor_copy(v_plane[:], tab_plane[:].indirect(offsets[:]))
         for cols in spans:
             nc.vector.tensor_copy(v_codes[:, cols], tab_codes[:].indirect(listed(cols)))
-        parts1 = sb.tile([P, 2 * width], BF16, name="parts1", align_bytes=64)
         nc.vector.tensor_single_scalar(
-            parts1[:, 0:width].bitcast(I32),
+            parts1[:, width : 2 * width].bitcast(I32),
             upper[:].rearrange("p n i -> p (n i)").bitcast(I32),
             HI_MASK_PAIR,
             ALU.bitwise_and,
         )
 
-        def gate_sum(u, cols, bank):
-            ga = ps.tile([P, cols.stop - cols.start], F32, name=bank)
+        def gate_sum(u, cols, ga):
             nc.tensor.matmul_mx(
-                out=ga[:],
+                out=ga,
                 lhsT=wg_codes[:, 2 * u * P : 2 * (u + 1) * P].bitcast(FP4X4),
                 lhsT_scale=wg_plane[:, u * P : (u + 1) * P],
                 rhs=v_codes[:, cols].bitcast(FP8X4),
@@ -135,12 +135,11 @@ def tile_list_hwayt_hl_gelu_kernel(
         def gate_tanh(u, ga, dest):
             nc.scalar.activation(dest, ga, ACT.Tanh, bias=half_bias[:, u : u + 1], scale=0.5)
 
-        def transform(u, bank):
-            ha = ps.tile([P, J], F32, name=bank)
+        def transform(u, ha):
             for part in range(2):
                 chans = slice(part * P, (part + 1) * P)
                 nc.tensor.matmul_mx(
-                    out=ha[:],
+                    out=ha,
                     lhsT=w_codes[u][:, chans].bitcast(FP8X4),
                     lhsT_scale=w_plane[u][:, chans],
                     rhs=v_codes[:].bitcast(FP8X4),
@@ -148,19 +147,21 @@ def tile_list_hwayt_hl_gelu_kernel(
                     start=(part == 0),
                     stop=(part == 1),
                 )
-            nc.scalar.activation(gelus[u][:], ha[:], ACT.Gelu_apprx_tanh)
+            nc.scalar.activation(gelus[u][:], ha, ACT.Gelu_apprx_tanh)
 
+        early = [ps.tile([P, 2 * J], F32, name="early0", tag="pair"), ps.tile([P, J], F32, name="early1", tag="single")]
         for half, cols in enumerate(spans):
-            gate_tanh(1, gate_sum(1, cols, "bank%d" % half)[:], tanh1[:, cols])
+            gate_tanh(1, gate_sum(1, cols, early[half][:, 0:HALF]), tanh1[:, cols])
             nc.scalar.activation(keep[:, cols], tanh1[:, cols], ACT.Identity, bias=0.5, scale=-0.5)
-        late_sum = gate_sum(0, whole, "bank2")
         quantise(0, parts0)
-        transform(0, "bank0")
+        pair = ps.tile([P, 2 * J], F32, name="pair", tag="pair")
+        transform(0, pair[:, 0:J])
+        late_sum = gate_sum(0, whole, pair[:, J : 2 * J])
         nc.vector.tensor_tensor(
-            by_word(parts1[:, width : 2 * width]), woven[1], by_word(parts1[:, 0:width]), ALU.subtract
+            by_word(parts1[:, 0:width]), woven[1], by_word(parts1[:, width : 2 * width]), ALU.subtract
         )
         quantise(1, parts1)
-        transform(1, "bank1")
+        transform(1, ps.tile([P, J], F32, name="single", tag="single")[:])
         nc.vector.tensor_tensor(carried[:, spans[0]], r_rows[1][:].indirect(listed(spans[0])), keep[:, spans[0]], ALU.mult)
         nc.vector.tensor_tensor(carried[:, spans[1]], r_rows[1][:].indirect(listed(spans[1])), keep[:, spans[1]], ALU.mult)
         for cols in spans:
@@ -173,7 +174,7 @@ def tile_list_hwayt_hl_gelu_kernel(
             nc.vector.scalar_tensor_tensor(scaled[:, cols], keep[:, cols], 1.0, diff[:, cols], ALU.subtract, ALU.mult)
 
         scale(ends[0])
-        nc.vector.scalar_tensor_tensor(result[1][:], made[:], 0.5, carried, ALU.mult, ALU.add)
+        nc.vector.scalar_tensor_tensor(result[1][:], made[:], 0.5, carried[:], ALU.mult, ALU.add)
         nc.sync.dma_start(out=out[P : 2 * P, :], in_=result[1][:])
         scale(ends[1])
         for cols in ends:

@@ -79,7 +79,7 @@ def tile_list_hwayt_hl_gelu_kernel(
         parts1 = parts[:, width : 3 * width]
         w_codes = tiles("w_codes", [P, 2 * P], U32)
         w_plane = tiles("w_plane", [P, 2 * P], U8)
-        tanh1 = sb.tile([P, J], F32, name="tanh1", align_bytes=64)
+        tanh = sb.tile([P, J], F32, name="tanh", align_bytes=64)
         gelus = tiles("gelu", [P, J], F32)
         result = tiles("result", [P, J], F32)
         keep = sb.tile([P, J], F32, name="keep", align_bytes=64)
@@ -149,32 +149,30 @@ def tile_list_hwayt_hl_gelu_kernel(
                 )
             nc.scalar.activation(gelus[u][:], ha, ACT.Gelu_apprx_tanh)
 
-        early = [ps.tile([P, 2 * J], F32, name="early0", tag="pair"), ps.tile([P, J], F32, name="early1", tag="single")]
         for half, cols in enumerate(spans):
-            gate_tanh(1, gate_sum(1, cols, early[half][:, 0:HALF]), tanh1[:, cols])
-            nc.scalar.activation(keep[:, cols], tanh1[:, cols], ACT.Identity, bias=0.5, scale=-0.5)
+            gate_tanh(1, gate_sum(1, cols, ps.tile([P, HALF], F32, name="bank%d" % half)[:]), tanh[:, cols])
+            nc.scalar.activation(keep[:, cols], tanh[:, cols], ACT.Identity, bias=0.5, scale=-0.5)
+        late_sum = gate_sum(0, whole, ps.tile([P, J], F32, name="bank2")[:])
+        for cols in spans:
+            gate_tanh(0, late_sum[:, cols], tanh[:, cols])
         quantise(0, parts0)
-        pair = ps.tile([P, 2 * J], F32, name="pair", tag="pair")
-        transform(0, pair[:, 0:J])
-        late_sum = gate_sum(0, whole, pair[:, J : 2 * J])
+        transform(0, ps.tile([P, J], F32, name="bank0")[:])
         nc.vector.tensor_tensor(
             by_word(parts1[:, 0:width]), woven[1], by_word(parts1[:, width : 2 * width]), ALU.subtract
         )
         quantise(1, parts1)
-        transform(1, ps.tile([P, J], F32, name="single", tag="single")[:])
+        transform(1, ps.tile([P, J], F32, name="bank1")[:])
         nc.vector.tensor_tensor(carried[:, spans[0]], r_rows[1][:].indirect(listed(spans[0])), keep[:, spans[0]], ALU.mult)
         nc.vector.tensor_tensor(carried[:, spans[1]], r_rows[1][:].indirect(listed(spans[1])), keep[:, spans[1]], ALU.mult)
-        for cols in spans:
-            gate_tanh(0, late_sum[:, cols], keep[:, cols])
         nc.vector.tensor_tensor(diff[:], r_rows[0][:].indirect(offsets[:]), gelus[0][:], ALU.subtract)
-        nc.vector.scalar_tensor_tensor(made[:], tanh1[:], 1.0, gelus[1][:], ALU.add, ALU.mult)
+        nc.vector.scalar_tensor_tensor(made[:], keep[:], 1.0, gelus[1][:], ALU.subtract, ALU.mult)
         ends = [slice(0, LONG), slice(LONG, J)]
 
         def scale(cols):
-            nc.vector.scalar_tensor_tensor(scaled[:, cols], keep[:, cols], 1.0, diff[:, cols], ALU.subtract, ALU.mult)
+            nc.vector.scalar_tensor_tensor(scaled[:, cols], tanh[:, cols], 1.0, diff[:, cols], ALU.subtract, ALU.mult)
 
         scale(ends[0])
-        nc.vector.scalar_tensor_tensor(result[1][:], made[:], 0.5, carried[:], ALU.mult, ALU.add)
+        nc.vector.tensor_tensor(result[1][:], carried[:], made[:], ALU.subtract)
         nc.sync.dma_start(out=out[P : 2 * P, :], in_=result[1][:])
         scale(ends[1])
         for cols in ends:

@@ -18,17 +18,18 @@ ACT = mybir.ActivationFunctionType
 
 P = 128
 PACK = 4
-TILES = N // P
-HI_MASK = 0xFFF00000 - (1 << 32)
+ROW_TILES = N // P
+WOVEN = P * PACK
 HALF = J // 2
 LONG = 320
+HI_MASK = 0xFFF00000 - (1 << 32)
 HI_MASK_PAIR = 0xFFF0FFF0 - (1 << 32)
 
 
-def load_scale_rows(queues, plane, rows):
+def load_scale_rows(nc, plane, rows):
     words = rows.bitcast(I32)
     for q in range(4):
-        queues[q].dma_start(out=plane[32 * q : 32 * q + 4, :].bitcast(I32), in_=words[4 * q : 4 * q + 4, :])
+        nc.sync.dma_start(out=plane[32 * q : 32 * q + 4, :].bitcast(I32), in_=words[4 * q : 4 * q + 4, :])
 
 
 def tile_list_hwayt_hl_gelu_kernel(
@@ -44,44 +45,45 @@ def tile_list_hwayt_hl_gelu_kernel(
         tab_codes = sb.tile([P, T], U32, name="tab_codes", align_bytes=64)
         wg_plane = sb.tile([P, N], U8, name="wg_plane", align_bytes=64)
         wg_codes = sb.tile([P, 2 * N], U8, name="wg_codes", align_bytes=64)
-        bias = sb.tile([P, TILES], F32, name="bias")
-        half_bias = sb.tile([P, TILES], F32, name="half_bias")
-        warm = sb.tile([P, 1], F32, name="warm")
-        warm_out = sb.tile([P, 1], F32, name="warm_out")
-        w_raw = [sb.tile([P, PACK, P], F32, name="w_raw%d" % u, align_bytes=64) for u in range(TILES)]
-        r_rows = [sb.tile([P, T], F32, name="r_rows%d" % u, align_bytes=64) for u in range(TILES)]
+        bias = sb.tile([P, ROW_TILES], F32, name="bias")
+        half_bias = sb.tile([P, ROW_TILES], F32, name="half_bias")
+        zero = sb.tile([P, 1], F32, name="zero")
+        gelu_bias = sb.tile([P, 1], F32, name="gelu_bias")
+        w_raw = [sb.tile([P, PACK, P], F32, name="w_raw%d" % u, align_bytes=64) for u in range(ROW_TILES)]
+        r_rows = [sb.tile([P, T], F32, name="r_rows%d" % u, align_bytes=64) for u in range(ROW_TILES)]
 
         nc.vector.memset(tab_plane[:].bitcast(I32), 0)
         nc.vector.memset(wg_plane[:].bitcast(I32), 0)
-        nc.vector.memset(warm[:], 0.0)
+        nc.gpsimd.memset(zero[:], 0.0)
+
+        nc.gpsimd.dma_start(out=wg_codes[:].bitcast(I32), in_=wg_words[0].bitcast(I32))
         w_rows = wh.rearrange("(p i) n -> p i n", i=PACK)
         nc.sync.dma_start(out=w_raw[0][:], in_=w_rows[:, :, 0:P])
         nc.sync.dma_start(offsets[:], offs)
-        load_scale_rows([nc.sync, nc.scalar, nc.sync, nc.scalar], tab_plane, tab_scales[0])
-        nc.scalar.activation(warm_out[:], warm[:], ACT.Gelu_apprx_tanh)
+        load_scale_rows(nc, tab_plane, tab_scales[0])
+        nc.scalar.activation(gelu_bias[:], zero[:], ACT.Gelu_apprx_tanh)
         nc.sync.dma_start(out=tab_codes[:].bitcast(I32), in_=tab_words[0].rearrange("p t i -> p (t i)").bitcast(I32))
         nc.sync.dma_start(out=w_raw[1][:], in_=w_rows[:, :, P : 2 * P])
-        nc.sync.dma_start(out=wg_codes[:].bitcast(I32), in_=wg_words[0].bitcast(I32))
-        load_scale_rows([nc.sync] * 4, wg_plane, wg_scales[0])
+        load_scale_rows(nc, wg_plane, wg_scales[0])
         with nc.allow_non_contiguous_dma(reason="one bias value a partition"):
             nc.sync.dma_start(out=bias[:], in_=bg.rearrange("(u p) -> p u", p=P))
         nc.sync.dma_start(out=r_rows[1][:], in_=rT[P : 2 * P, :])
         nc.sync.dma_start(out=r_rows[0][:], in_=rT[0:P, :])
 
-        def tiles(name, shape, dtype):
-            return [sb.tile(shape, dtype, name="%s%d" % (name, u), align_bytes=64) for u in range(TILES)]
+        def per_row_tile(name, shape, dtype):
+            return [sb.tile(shape, dtype, name="%s%d" % (name, u), align_bytes=64) for u in range(ROW_TILES)]
 
-        width = P * PACK
         hi32 = sb.tile([P, P, PACK], F32, name="hi32", align_bytes=64)
         upper = sb.tile([P, P, PACK], BF16, name="upper", align_bytes=64)
-        parts = sb.tile([P, 3 * width], BF16, name="parts", align_bytes=64)
-        parts0 = parts[:, 0 : 2 * width]
-        parts1 = parts[:, width : 3 * width]
-        w_codes = tiles("w_codes", [P, 2 * P], U32)
-        w_plane = tiles("w_plane", [P, 2 * P], U8)
+        staging = sb.tile([P, 3 * WOVEN], BF16, name="staging", align_bytes=64)
+        staged = [staging[:, u * WOVEN : (u + 2) * WOVEN] for u in range(ROW_TILES)]
+        hi = [staging[:, 2 * u * WOVEN : (2 * u + 1) * WOVEN] for u in range(ROW_TILES)]
+        lo = staging[:, WOVEN : 2 * WOVEN]
+        w_codes = per_row_tile("w_codes", [P, 2 * P], U32)
+        w_plane = per_row_tile("w_plane", [P, 2 * P], U8)
         tanh = sb.tile([P, J], F32, name="tanh", align_bytes=64)
-        gelus = tiles("gelu", [P, J], F32)
-        result = tiles("result", [P, J], F32)
+        gelus = per_row_tile("gelu", [P, J], F32)
+        result = per_row_tile("result", [P, J], F32)
         keep = sb.tile([P, J], F32, name="keep", align_bytes=64)
         made = sb.tile([P, J], F32, name="made", align_bytes=64)
         diff = sb.tile([P, J], F32, name="diff", align_bytes=64)
@@ -89,9 +91,9 @@ def tile_list_hwayt_hl_gelu_kernel(
         carried = sb.tile([P, J], F32, name="carried", align_bytes=64)
         v_plane = sb.tile([P, J], U8, name="v_plane", align_bytes=64)
         v_codes = sb.tile([P, J], U32, name="v_codes", align_bytes=64)
-        woven = [w_raw[u][:].rearrange("p i n -> p n i") for u in range(TILES)]
-        spans = [slice(0, HALF), slice(HALF, J)]
-        whole = slice(0, J)
+        woven = [w_raw[u][:].rearrange("p i n -> p n i") for u in range(ROW_TILES)]
+        halves = [slice(0, HALF), slice(HALF, J)]
+        ends = [slice(0, LONG), slice(LONG, J)]
 
         def listed(cols):
             return offsets[:, cols.start // 16 : cols.stop // 16]
@@ -99,25 +101,22 @@ def tile_list_hwayt_hl_gelu_kernel(
         def by_word(ap):
             return ap.rearrange("p (n i) -> p n i", i=PACK)
 
-        def quantise(u, staged):
-            nc.vector.quantize_mx(out=w_codes[u][:].bitcast(FP8X4), scales=w_plane[u][:], in_=staged)
+        def quantise(u):
+            nc.vector.quantize_mx(out=w_codes[u][:].bitcast(FP8X4), scales=w_plane[u][:], in_=staged[u])
 
         nc.vector.tensor_single_scalar(
             hi32[:].bitcast(I32), w_raw[0][:].bitcast(I32).rearrange("p i n -> p n i"), HI_MASK, ALU.bitwise_and
         )
-        nc.gpsimd.tensor_tensor(by_word(parts0[:, width : 2 * width]), woven[0], hi32[:], ALU.subtract)
-        halves = w_raw[1][:].bitcast(BF16).rearrange("p i (n h) -> p n i h", h=2)
-        nc.scalar.copy(parts0[:, 0:width], hi32[:].rearrange("p n i -> p (n i)"))
-        nc.scalar.copy(upper[:], halves[:, :, :, 1])
+        nc.gpsimd.tensor_tensor(by_word(lo), woven[0], hi32[:], ALU.subtract)
+        nc.scalar.copy(hi[0], hi32[:].rearrange("p n i -> p (n i)"))
+        word_halves = w_raw[1][:].bitcast(BF16).rearrange("p i (n h) -> p n i h", h=2)
+        nc.scalar.copy(upper[:], word_halves[:, :, :, 1])
         nc.scalar.mul(half_bias[:], bias[:], 0.5)
         nc.vector.tensor_copy(v_plane[:], tab_plane[:].indirect(offsets[:]))
-        for cols in spans:
+        for cols in halves:
             nc.vector.tensor_copy(v_codes[:, cols], tab_codes[:].indirect(listed(cols)))
         nc.vector.tensor_single_scalar(
-            parts1[:, width : 2 * width].bitcast(I32),
-            upper[:].rearrange("p n i -> p (n i)").bitcast(I32),
-            HI_MASK_PAIR,
-            ALU.bitwise_and,
+            hi[1].bitcast(I32), upper[:].rearrange("p n i -> p (n i)").bitcast(I32), HI_MASK_PAIR, ALU.bitwise_and
         )
 
         def gate_sum(u, cols, ga):
@@ -130,10 +129,9 @@ def tile_list_hwayt_hl_gelu_kernel(
                 start=True,
                 stop=True,
             )
-            return ga
 
-        def gate_tanh(u, ga, dest):
-            nc.scalar.activation(dest, ga, ACT.Tanh, bias=half_bias[:, u : u + 1], scale=0.5)
+        def gate_tanh(u, cols, ga):
+            nc.scalar.activation(tanh[:, cols], ga, ACT.Tanh, bias=half_bias[:, u : u + 1], scale=0.5)
 
         def transform(u, ha):
             for part in range(2):
@@ -147,26 +145,27 @@ def tile_list_hwayt_hl_gelu_kernel(
                     start=(part == 0),
                     stop=(part == 1),
                 )
-            nc.scalar.activation(gelus[u][:], ha, ACT.Gelu_apprx_tanh)
+            nc.scalar.activation(gelus[u][:], ha, ACT.Gelu_apprx_tanh, bias=gelu_bias[:])
 
-        for half, cols in enumerate(spans):
-            gate_tanh(1, gate_sum(1, cols, ps.tile([P, HALF], F32, name="bank%d" % half)[:]), tanh[:, cols])
+        for half, cols in enumerate(halves):
+            ga_half = ps.tile([P, HALF], F32, name="bank%d" % half)
+            gate_sum(1, cols, ga_half[:])
+            gate_tanh(1, cols, ga_half[:])
             nc.scalar.activation(keep[:, cols], tanh[:, cols], ACT.Identity, bias=0.5, scale=-0.5)
-        late_sum = gate_sum(0, whole, ps.tile([P, J], F32, name="bank2")[:])
-        for cols in spans:
-            gate_tanh(0, late_sum[:, cols], tanh[:, cols])
-        quantise(0, parts0)
+        ga_whole = ps.tile([P, J], F32, name="bank2")
+        gate_sum(0, slice(0, J), ga_whole[:])
+        for cols in halves:
+            gate_tanh(0, cols, ga_whole[:, cols])
+        quantise(0)
         transform(0, ps.tile([P, J], F32, name="bank0")[:])
-        nc.vector.tensor_tensor(
-            by_word(parts1[:, 0:width]), woven[1], by_word(parts1[:, width : 2 * width]), ALU.subtract
-        )
-        quantise(1, parts1)
+        nc.vector.tensor_tensor(by_word(lo), woven[1], by_word(hi[1]), ALU.subtract)
+        quantise(1)
         transform(1, ps.tile([P, J], F32, name="bank1")[:])
-        nc.vector.tensor_tensor(carried[:, spans[0]], r_rows[1][:].indirect(listed(spans[0])), keep[:, spans[0]], ALU.mult)
-        nc.vector.tensor_tensor(carried[:, spans[1]], r_rows[1][:].indirect(listed(spans[1])), keep[:, spans[1]], ALU.mult)
+
+        for cols in halves:
+            nc.vector.tensor_tensor(carried[:, cols], r_rows[1][:].indirect(listed(cols)), keep[:, cols], ALU.mult)
         nc.vector.tensor_tensor(diff[:], r_rows[0][:].indirect(offsets[:]), gelus[0][:], ALU.subtract)
         nc.vector.scalar_tensor_tensor(made[:], keep[:], 1.0, gelus[1][:], ALU.subtract, ALU.mult)
-        ends = [slice(0, LONG), slice(LONG, J)]
 
         def scale(cols):
             nc.vector.scalar_tensor_tensor(scaled[:, cols], tanh[:, cols], 1.0, diff[:, cols], ALU.subtract, ALU.mult)

@@ -22,6 +22,7 @@ ROW_TILES = N // P
 WOVEN = P * PACK
 HALF = J // 2
 LONG = 320
+BANK = 2048
 HI_MASK = 0xFFF00000 - (1 << 32)
 HI_MASK_PAIR = 0xFFF0FFF0 - (1 << 32)
 
@@ -75,17 +76,16 @@ def tile_list_hwayt_hl_gelu_kernel(
 
         hi32 = sb.tile([P, P, PACK], F32, name="hi32", align_bytes=64)
         upper = sb.tile([P, P, PACK], BF16, name="upper", align_bytes=64)
-        staging = sb.tile([P, 3 * WOVEN], BF16, name="staging", align_bytes=64)
-        staged = [staging[:, u * WOVEN : (u + 2) * WOVEN] for u in range(ROW_TILES)]
-        hi = [staging[:, 2 * u * WOVEN : (2 * u + 1) * WOVEN] for u in range(ROW_TILES)]
-        lo = staging[:, WOVEN : 2 * WOVEN]
-        w_codes = per_row_tile("w_codes", [P, 2 * P], U32)
-        w_plane = per_row_tile("w_plane", [P, 2 * P], U8)
+        staging = sb.tile([P, 2 * WOVEN], BF16, name="staging", align_bytes=64)
+        lo1 = sb.tile([P, WOVEN], BF16, name="lo1", align_bytes=64)
+        codes0 = sb.tile([P, 2 * P], U32, name="codes0", align_bytes=64)
+        plane0 = sb.tile([P, 2 * P], U8, name="plane0", align_bytes=64)
+        codes1 = [sb.tile([P, P], U32, name="codes1_%d" % part, align_bytes=64) for part in range(2)]
+        plane1 = [sb.tile([P, P], U8, name="plane1_%d" % part, align_bytes=64) for part in range(2)]
         tanh = sb.tile([P, J], F32, name="tanh", align_bytes=64)
         gelus = per_row_tile("gelu", [P, J], F32)
         result = per_row_tile("result", [P, J], F32)
         keep = sb.tile([P, J], F32, name="keep", align_bytes=64)
-        made = sb.tile([P, J], F32, name="made", align_bytes=64)
         diff = sb.tile([P, J], F32, name="diff", align_bytes=64)
         scaled = sb.tile([P, J], F32, name="scaled", align_bytes=64)
         carried = sb.tile([P, J], F32, name="carried", align_bytes=64)
@@ -101,22 +101,23 @@ def tile_list_hwayt_hl_gelu_kernel(
         def by_word(ap):
             return ap.rearrange("p (n i) -> p n i", i=PACK)
 
-        def quantise(u):
-            nc.vector.quantize_mx(out=w_codes[u][:].bitcast(FP8X4), scales=w_plane[u][:], in_=staged[u])
+        def quantise(codes, plane, values):
+            nc.vector.quantize_mx(out=codes.bitcast(FP8X4), scales=plane, in_=values)
 
         nc.vector.tensor_single_scalar(
             hi32[:].bitcast(I32), w_raw[0][:].bitcast(I32).rearrange("p i n -> p n i"), HI_MASK, ALU.bitwise_and
         )
-        nc.gpsimd.tensor_tensor(by_word(lo), woven[0], hi32[:], ALU.subtract)
-        nc.scalar.copy(hi[0], hi32[:].rearrange("p n i -> p (n i)"))
+        nc.gpsimd.tensor_tensor(by_word(staging[:, WOVEN:]), woven[0], hi32[:], ALU.subtract)
+        nc.scalar.copy(staging[:, :WOVEN], hi32[:].rearrange("p n i -> p (n i)"))
         word_halves = w_raw[1][:].bitcast(BF16).rearrange("p i (n h) -> p n i h", h=2)
         nc.scalar.copy(upper[:], word_halves[:, :, :, 1])
         nc.scalar.mul(half_bias[:], bias[:], 0.5)
         nc.vector.tensor_copy(v_plane[:], tab_plane[:].indirect(offsets[:]))
         for cols in halves:
             nc.vector.tensor_copy(v_codes[:, cols], tab_codes[:].indirect(listed(cols)))
+        hi1 = sb.tile([P, WOVEN], BF16, name="hi32", align_bytes=64)
         nc.vector.tensor_single_scalar(
-            hi[1].bitcast(I32), upper[:].rearrange("p n i -> p (n i)").bitcast(I32), HI_MASK_PAIR, ALU.bitwise_and
+            hi1[:].bitcast(I32), upper[:].rearrange("p n i -> p (n i)").bitcast(I32), HI_MASK_PAIR, ALU.bitwise_and
         )
 
         def gate_sum(u, cols, ga):
@@ -133,13 +134,12 @@ def tile_list_hwayt_hl_gelu_kernel(
         def gate_tanh(u, cols, ga):
             nc.scalar.activation(tanh[:, cols], ga, ACT.Tanh, bias=half_bias[:, u : u + 1], scale=0.5)
 
-        def transform(u, ha):
-            for part in range(2):
-                chans = slice(part * P, (part + 1) * P)
+        def transform(u, parts, ha):
+            for part, (codes, plane) in enumerate(parts):
                 nc.tensor.matmul_mx(
                     out=ha,
-                    lhsT=w_codes[u][:, chans].bitcast(FP8X4),
-                    lhsT_scale=w_plane[u][:, chans],
+                    lhsT=codes.bitcast(FP8X4),
+                    lhsT_scale=plane,
                     rhs=v_codes[:].bitcast(FP8X4),
                     rhs_scale=v_plane[:],
                     start=(part == 0),
@@ -148,32 +148,32 @@ def tile_list_hwayt_hl_gelu_kernel(
             nc.scalar.activation(gelus[u][:], ha, ACT.Gelu_apprx_tanh, bias=gelu_bias[:])
 
         for half, cols in enumerate(halves):
-            ga_half = ps.tile([P, HALF], F32, name="bank%d" % half)
-            gate_sum(1, cols, ga_half[:])
-            gate_tanh(1, cols, ga_half[:])
+            ga_half = ps.tile([P, (1 + half) * J], F32, name="ga_half%d" % half, offset=half * BANK)[:, :HALF]
+            gate_sum(1, cols, ga_half)
+            gate_tanh(1, cols, ga_half)
             nc.scalar.activation(keep[:, cols], tanh[:, cols], ACT.Identity, bias=0.5, scale=-0.5)
-        ga_whole = ps.tile([P, J], F32, name="bank2")
-        gate_sum(0, slice(0, J), ga_whole[:])
-        for cols in halves:
-            gate_tanh(0, cols, ga_whole[:, cols])
-        quantise(0)
-        transform(0, ps.tile([P, J], F32, name="bank0")[:])
-        nc.vector.tensor_tensor(by_word(lo), woven[1], by_word(hi[1]), ALU.subtract)
-        quantise(1)
-        transform(1, ps.tile([P, J], F32, name="bank1")[:])
+        quantise(codes0[:], plane0[:], staging[:])
+        transform(0, [(codes0[:, c], plane0[:, c]) for c in (slice(0, P), slice(P, 2 * P))], ps.tile([P, J], F32, name="ha0", offset=0)[:])
+        ga0 = ps.tile([P, J], F32, name="ga0", offset=BANK)
+        gate_sum(0, slice(0, J), ga0[:])
+        gate_tanh(0, slice(0, J), ga0[:])
+        nc.vector.tensor_tensor(by_word(lo1[:]), woven[1], by_word(hi1[:]), ALU.subtract)
+        quantise(codes1[0][:], plane1[0][:], hi1[:])
+        quantise(codes1[1][:], plane1[1][:], lo1[:])
+        transform(1, [(codes1[part][:], plane1[part][:]) for part in range(2)], ps.tile([P, J], F32, name="ha1", offset=2 * BANK)[:])
 
         for cols in halves:
             nc.vector.tensor_tensor(carried[:, cols], r_rows[1][:].indirect(listed(cols)), keep[:, cols], ALU.mult)
-        nc.vector.tensor_tensor(diff[:], r_rows[0][:].indirect(offsets[:]), gelus[0][:], ALU.subtract)
-        nc.vector.scalar_tensor_tensor(made[:], keep[:], 1.0, gelus[1][:], ALU.subtract, ALU.mult)
-
-        def scale(cols):
+        for cols in halves:
+            nc.vector.tensor_tensor(diff[:, cols], r_rows[0][:].indirect(listed(cols)), gelus[0][:, cols], ALU.subtract)
+        for cols in halves:
             nc.vector.scalar_tensor_tensor(scaled[:, cols], tanh[:, cols], 1.0, diff[:, cols], ALU.subtract, ALU.mult)
-
-        scale(ends[0])
-        nc.vector.tensor_tensor(result[1][:], carried[:], made[:], ALU.subtract)
-        nc.sync.dma_start(out=out[P : 2 * P, :], in_=result[1][:])
-        scale(ends[1])
-        for cols in ends:
+        for cols in halves:
             nc.vector.scalar_tensor_tensor(result[0][:, cols], scaled[:, cols], -0.5, gelus[0][:, cols], ALU.mult, ALU.add)
-            nc.sync.dma_start(out=out[0:P, cols], in_=result[0][:, cols])
+        nc.sync.dma_start(out=out[0:P, :], in_=result[0][:])
+        made = diff
+        for cols in ends:
+            nc.vector.scalar_tensor_tensor(made[:, cols], keep[:, cols], 1.0, gelus[1][:, cols], ALU.subtract, ALU.mult)
+        for cols in ends:
+            nc.vector.tensor_tensor(result[1][:, cols], carried[:, cols], made[:, cols], ALU.subtract)
+            nc.sync.dma_start(out=out[P : 2 * P, cols], in_=result[1][:, cols])

@@ -22,15 +22,14 @@ ROW_TILES = N // P
 WOVEN = P * PACK
 HALF = J // 2
 LONG = 320
-BANK = 2048
 HI_MASK = 0xFFF00000 - (1 << 32)
 HI_MASK_PAIR = 0xFFF0FFF0 - (1 << 32)
 
 
-def load_scale_rows(nc, plane, rows):
+def load_scale_rows(queues, plane, rows):
     words = rows.bitcast(I32)
     for q in range(4):
-        nc.sync.dma_start(out=plane[32 * q : 32 * q + 4, :].bitcast(I32), in_=words[4 * q : 4 * q + 4, :])
+        queues[q % len(queues)].dma_start(out=plane[32 * q : 32 * q + 4, :].bitcast(I32), in_=words[4 * q : 4 * q + 4, :])
 
 
 def tile_list_hwayt_hl_gelu_kernel(
@@ -54,18 +53,18 @@ def tile_list_hwayt_hl_gelu_kernel(
         r_rows = [sb.tile([P, T], F32, name="r_rows%d" % u, align_bytes=64) for u in range(ROW_TILES)]
 
         nc.vector.memset(tab_plane[:].bitcast(I32), 0)
-        nc.vector.memset(wg_plane[:].bitcast(I32), 0)
         nc.gpsimd.memset(zero[:], 0.0)
+        nc.vector.memset(wg_plane[:].bitcast(I32), 0)
 
         nc.gpsimd.dma_start(out=wg_codes[:].bitcast(I32), in_=wg_words[0].bitcast(I32))
         w_rows = wh.rearrange("(p i) n -> p i n", i=PACK)
         nc.sync.dma_start(out=w_raw[0][:], in_=w_rows[:, :, 0:P])
         nc.sync.dma_start(offsets[:], offs)
-        load_scale_rows(nc, tab_plane, tab_scales[0])
+        load_scale_rows([nc.sync], tab_plane, tab_scales[0])
         nc.scalar.activation(gelu_bias[:], zero[:], ACT.Gelu_apprx_tanh)
         nc.sync.dma_start(out=tab_codes[:].bitcast(I32), in_=tab_words[0].rearrange("p t i -> p (t i)").bitcast(I32))
         nc.sync.dma_start(out=w_raw[1][:], in_=w_rows[:, :, P : 2 * P])
-        load_scale_rows(nc, wg_plane, wg_scales[0])
+        load_scale_rows([nc.sync], wg_plane, wg_scales[0])
         with nc.allow_non_contiguous_dma(reason="one bias value a partition"):
             nc.sync.dma_start(out=bias[:], in_=bg.rearrange("(u p) -> p u", p=P))
         nc.sync.dma_start(out=r_rows[1][:], in_=rT[P : 2 * P, :])
@@ -81,14 +80,13 @@ def tile_list_hwayt_hl_gelu_kernel(
         codes0 = sb.tile([P, 2 * P], U32, name="codes0", align_bytes=64)
         plane0 = sb.tile([P, 2 * P], U8, name="plane0", align_bytes=64)
         codes1 = [sb.tile([P, P], U32, name="codes1_%d" % part, align_bytes=64) for part in range(2)]
-        plane1 = [sb.tile([P, P], U8, name="plane1_%d" % part, align_bytes=64) for part in range(2)]
+        plane1 = [sb.tile([P, P], U8, name="plane1_%d" % part, align_bytes=64)[:] for part in range(2)]
         tanh = sb.tile([P, J], F32, name="tanh", align_bytes=64)
         gelus = per_row_tile("gelu", [P, J], F32)
         result = per_row_tile("result", [P, J], F32)
         keep = sb.tile([P, J], F32, name="keep", align_bytes=64)
         diff = sb.tile([P, J], F32, name="diff", align_bytes=64)
         scaled = sb.tile([P, J], F32, name="scaled", align_bytes=64)
-        carried = sb.tile([P, J], F32, name="carried", align_bytes=64)
         v_plane = sb.tile([P, J], U8, name="v_plane", align_bytes=64)
         v_codes = sb.tile([P, J], U32, name="v_codes", align_bytes=64)
         woven = [w_raw[u][:].rearrange("p i n -> p n i") for u in range(ROW_TILES)]
@@ -147,33 +145,32 @@ def tile_list_hwayt_hl_gelu_kernel(
                 )
             nc.scalar.activation(gelus[u][:], ha, ACT.Gelu_apprx_tanh, bias=gelu_bias[:])
 
-        for half, cols in enumerate(halves):
-            ga_half = ps.tile([P, (1 + half) * J], F32, name="ga_half%d" % half, offset=half * BANK)[:, :HALF]
-            gate_sum(1, cols, ga_half)
-            gate_tanh(1, cols, ga_half)
-            nc.scalar.activation(keep[:, cols], tanh[:, cols], ACT.Identity, bias=0.5, scale=-0.5)
+        for cols, bank in ((slice(0, P), "bank0"), (slice(P, HALF), "bank2"), (halves[1], "bank1")):
+            ga_part = ps.tile([P, cols.stop - cols.start], F32, name=bank)[:]
+            gate_sum(1, cols, ga_part)
+            gate_tanh(1, cols, ga_part)
+            if cols.stop % HALF == 0:
+                done = slice(cols.stop - HALF, cols.stop)
+                nc.scalar.activation(keep[:, done], tanh[:, done], ACT.Identity, bias=0.5, scale=-0.5)
         quantise(codes0[:], plane0[:], staging[:])
-        transform(0, [(codes0[:, c], plane0[:, c]) for c in (slice(0, P), slice(P, 2 * P))], ps.tile([P, J], F32, name="ha0", offset=0)[:])
-        ga0 = ps.tile([P, J], F32, name="ga0", offset=BANK)
+        transform(0, [(codes0[:, c], plane0[:, c]) for c in (slice(0, P), slice(P, 2 * P))], ps.tile([P, J], F32, name="bank0")[:])
+        nc.vector.tensor_tensor(by_word(lo1[:]), woven[1], by_word(hi1[:]), ALU.subtract)
+        quantise(codes1[0][:], plane1[0], hi1[:])
+        quantise(codes1[1][:], plane1[1], lo1[:])
+        transform(1, [(codes1[part][:], plane1[part]) for part in range(2)], ps.tile([P, J], F32, name="bank1")[:])
+        ga0 = ps.tile([P, J], F32, name="bank0")
         gate_sum(0, slice(0, J), ga0[:])
         gate_tanh(0, slice(0, J), ga0[:])
-        nc.vector.tensor_tensor(by_word(lo1[:]), woven[1], by_word(hi1[:]), ALU.subtract)
-        quantise(codes1[0][:], plane1[0][:], hi1[:])
-        quantise(codes1[1][:], plane1[1][:], lo1[:])
-        transform(1, [(codes1[part][:], plane1[part][:]) for part in range(2)], ps.tile([P, J], F32, name="ha1", offset=2 * BANK)[:])
 
+        carried = sb.tile([P, J], F32, name="w_raw1", align_bytes=64)
         for cols in halves:
             nc.vector.tensor_tensor(carried[:, cols], r_rows[1][:].indirect(listed(cols)), keep[:, cols], ALU.mult)
+        nc.vector.tensor_tensor(diff[:], r_rows[0][:].indirect(offsets[:]), gelus[0][:], ALU.subtract)
+        made = sb.tile([P, J], F32, name="made", align_bytes=64)
+        nc.vector.scalar_tensor_tensor(made[:], keep[:], 1.0, gelus[1][:], ALU.subtract, ALU.mult)
+        nc.vector.scalar_tensor_tensor(scaled[:], tanh[:], 1.0, diff[:], ALU.subtract, ALU.mult)
         for cols in halves:
-            nc.vector.tensor_tensor(diff[:, cols], r_rows[0][:].indirect(listed(cols)), gelus[0][:, cols], ALU.subtract)
-        for cols in halves:
-            nc.vector.scalar_tensor_tensor(scaled[:, cols], tanh[:, cols], 1.0, diff[:, cols], ALU.subtract, ALU.mult)
-        for cols in halves:
-            nc.vector.scalar_tensor_tensor(result[0][:, cols], scaled[:, cols], -0.5, gelus[0][:, cols], ALU.mult, ALU.add)
-        nc.sync.dma_start(out=out[0:P, :], in_=result[0][:])
-        made = diff
-        for cols in ends:
-            nc.vector.scalar_tensor_tensor(made[:, cols], keep[:, cols], 1.0, gelus[1][:, cols], ALU.subtract, ALU.mult)
-        for cols in ends:
             nc.vector.tensor_tensor(result[1][:, cols], carried[:, cols], made[:, cols], ALU.subtract)
             nc.sync.dma_start(out=out[P : 2 * P, cols], in_=result[1][:, cols])
+            nc.vector.scalar_tensor_tensor(result[0][:, cols], scaled[:, cols], -0.5, gelus[0][:, cols], ALU.mult, ALU.add)
+            nc.sync.dma_start(out=out[0:P, cols], in_=result[0][:, cols])

@@ -143,7 +143,8 @@ def tile_list_hwayt_hl_gelu_kernel(
                     start=(part == 0),
                     stop=(part == 1),
                 )
-            nc.scalar.activation(gelus[u][:], ha, ACT.Gelu_apprx_tanh, bias=gelu_bias[:])
+            for cols in halves:
+                nc.scalar.activation(gelus[u][:, cols], ha[:, cols], ACT.Gelu_apprx_tanh, bias=gelu_bias[:])
 
         for cols, bank in ((slice(0, P), "bank0"), (slice(P, HALF), "bank2"), (halves[1], "bank1")):
             ga_part = ps.tile([P, cols.stop - cols.start], F32, name=bank)[:]
@@ -165,12 +166,16 @@ def tile_list_hwayt_hl_gelu_kernel(
         carried = sb.tile([P, J], F32, name="w_raw1", align_bytes=64)
         for cols in halves:
             nc.vector.tensor_tensor(carried[:, cols], r_rows[1][:].indirect(listed(cols)), keep[:, cols], ALU.mult)
-        nc.vector.tensor_tensor(diff[:], r_rows[0][:].indirect(offsets[:]), gelus[0][:], ALU.subtract)
+        for cols in halves:
+            nc.vector.tensor_tensor(diff[:, cols], r_rows[0][:].indirect(listed(cols)), gelus[0][:, cols], ALU.subtract)
         made = sb.tile([P, J], F32, name="made", align_bytes=64)
-        nc.vector.scalar_tensor_tensor(made[:], keep[:], 1.0, gelus[1][:], ALU.subtract, ALU.mult)
-        nc.vector.scalar_tensor_tensor(scaled[:], tanh[:], 1.0, diff[:], ALU.subtract, ALU.mult)
+        for cols in halves:
+            nc.vector.scalar_tensor_tensor(made[:, cols], keep[:, cols], 1.0, gelus[1][:, cols], ALU.subtract, ALU.mult)
         for cols in halves:
             nc.vector.tensor_tensor(result[1][:, cols], carried[:, cols], made[:, cols], ALU.subtract)
             nc.sync.dma_start(out=out[P : 2 * P, cols], in_=result[1][:, cols])
+        for cols in halves:
+            nc.vector.scalar_tensor_tensor(scaled[:, cols], tanh[:, cols], 1.0, diff[:, cols], ALU.subtract, ALU.mult)
+        for cols in halves:
             nc.vector.scalar_tensor_tensor(result[0][:, cols], scaled[:, cols], -0.5, gelus[0][:, cols], ALU.mult, ALU.add)
             nc.sync.dma_start(out=out[0:P, cols], in_=result[0][:, cols])

@@ -102,13 +102,19 @@ def tile_list_hwayt_hl_gelu_kernel(
         def quantise(codes, plane, values):
             nc.vector.quantize_mx(out=codes.bitcast(FP8X4), scales=plane, in_=values)
 
+        def rows_by_pairs(ap):
+            return ap.rearrange("p i (c e) -> p c i e", e=2)
+
+        def words_by_pairs(ap):
+            return ap.rearrange("p (c e) i -> p c i e", e=2)
+
         nc.vector.tensor_single_scalar(
-            hi32[:].bitcast(I32), w_raw[0][:].bitcast(I32).rearrange("p i n -> p n i"), HI_MASK, ALU.bitwise_and
+            words_by_pairs(hi32[:].bitcast(I32)), rows_by_pairs(w_raw[0][:].bitcast(I32)), HI_MASK, ALU.bitwise_and
         )
         nc.gpsimd.tensor_tensor(by_word(staging[:, WOVEN:]), woven[0], hi32[:], ALU.subtract)
         nc.scalar.copy(staging[:, :WOVEN], hi32[:].rearrange("p n i -> p (n i)"))
-        word_halves = w_raw[1][:].bitcast(BF16).rearrange("p i (n h) -> p n i h", h=2)
-        nc.scalar.copy(upper[:], word_halves[:, :, :, 1])
+        word_halves = w_raw[1][:].bitcast(BF16).rearrange("p i (n h) -> p i n h", h=2)
+        nc.scalar.copy(words_by_pairs(upper[:]), rows_by_pairs(word_halves[:, :, :, 1]))
         nc.scalar.mul(half_bias[:], bias[:], 0.5)
         nc.vector.tensor_copy(v_plane[:], tab_plane[:].indirect(offsets[:]))
         for cols in halves:
@@ -155,7 +161,9 @@ def tile_list_hwayt_hl_gelu_kernel(
                 nc.scalar.activation(keep[:, done], tanh[:, done], ACT.Identity, bias=0.5, scale=-0.5)
         quantise(codes0[:], plane0[:], staging[:])
         transform(0, [(codes0[:, c], plane0[:, c]) for c in (slice(0, P), slice(P, 2 * P))], ps.tile([P, J], F32, name="bank0")[:])
-        nc.vector.tensor_tensor(by_word(lo1[:]), woven[1], by_word(hi1[:]), ALU.subtract)
+        nc.vector.tensor_tensor(
+            words_by_pairs(by_word(lo1[:])), rows_by_pairs(w_raw[1][:]), words_by_pairs(by_word(hi1[:])), ALU.subtract
+        )
         quantise(codes1[0][:], plane1[0], hi1[:])
         quantise(codes1[1][:], plane1[1], lo1[:])
         transform(1, [(codes1[part][:], plane1[part]) for part in range(2)], ps.tile([P, J], F32, name="bank1")[:])

@@ -52,13 +52,13 @@ def tile_list_hwayt_hl_gelu_kernel(
         w_raw = [sb.tile([P, PACK, P], F32, name="w_raw%d" % u, align_bytes=64) for u in range(ROW_TILES)]
         r_rows = [sb.tile([P, T], F32, name="r_rows%d" % u, align_bytes=64) for u in range(ROW_TILES)]
 
-        nc.vector.memset(tab_plane[:].bitcast(I32), 0)
+        nc.gpsimd.memset(tab_plane[:].bitcast(I32), 0)
         nc.gpsimd.memset(zero[:], 0.0)
         nc.vector.memset(wg_plane[:].bitcast(I32), 0)
 
         nc.gpsimd.dma_start(out=wg_codes[:].bitcast(I32), in_=wg_words[0].bitcast(I32))
         w_rows = wh.rearrange("(p i) n -> p i n", i=PACK)
-        nc.sync.dma_start(out=w_raw[0][:], in_=w_rows[:, :, 0:P])
+        nc.scalar.dma_start(out=w_raw[0][:], in_=w_rows[:, :, 0:P])
         nc.sync.dma_start(offsets[:], offs)
         load_scale_rows([nc.sync], tab_plane, tab_scales[0])
         nc.scalar.activation(gelu_bias[:], zero[:], ACT.Gelu_apprx_tanh)
@@ -81,12 +81,9 @@ def tile_list_hwayt_hl_gelu_kernel(
         plane0 = sb.tile([P, 2 * P], U8, name="plane0", align_bytes=64)
         codes1 = [sb.tile([P, P], U32, name="codes1_%d" % part, align_bytes=64) for part in range(2)]
         plane1 = [sb.tile([P, P], U8, name="plane1_%d" % part, align_bytes=64)[:] for part in range(2)]
-        tanh = sb.tile([P, J], F32, name="tanh", align_bytes=64)
-        gelus = per_row_tile("gelu", [P, J], F32)
         result = per_row_tile("result", [P, J], F32)
-        keep = sb.tile([P, J], F32, name="keep", align_bytes=64)
-        diff = sb.tile([P, J], F32, name="diff", align_bytes=64)
-        scaled = sb.tile([P, J], F32, name="scaled", align_bytes=64)
+        keep = per_row_tile("keep", [P, J], F32)
+        made = per_row_tile("made", [P, J], F32)
         v_plane = sb.tile([P, J], U8, name="v_plane", align_bytes=64)
         v_codes = sb.tile([P, J], U32, name="v_codes", align_bytes=64)
         woven = [w_raw[u][:].rearrange("p i n -> p n i") for u in range(ROW_TILES)]
@@ -102,6 +99,8 @@ def tile_list_hwayt_hl_gelu_kernel(
         def quantise(codes, plane, values):
             nc.vector.quantize_mx(out=codes.bitcast(FP8X4), scales=plane, in_=values)
 
+        nc.vector.tensor_copy(v_plane[:, halves[0]], tab_plane[:].indirect(listed(halves[0])))
+
         def rows_by_pairs(ap):
             return ap.rearrange("p i (c e) -> p c i e", e=2)
 
@@ -116,7 +115,7 @@ def tile_list_hwayt_hl_gelu_kernel(
         word_halves = w_raw[1][:].bitcast(BF16).rearrange("p i (n h) -> p i n h", h=2)
         nc.scalar.copy(words_by_pairs(upper[:]), rows_by_pairs(word_halves[:, :, :, 1]))
         nc.scalar.mul(half_bias[:], bias[:], 0.5)
-        nc.vector.tensor_copy(v_plane[:], tab_plane[:].indirect(offsets[:]))
+        nc.vector.tensor_copy(v_plane[:, halves[1]], tab_plane[:].indirect(listed(halves[1])))
         for cols in halves:
             nc.vector.tensor_copy(v_codes[:, cols], tab_codes[:].indirect(listed(cols)))
         hi1 = sb.tile([P, WOVEN], BF16, name="hi32", align_bytes=64)
@@ -135,10 +134,7 @@ def tile_list_hwayt_hl_gelu_kernel(
                 stop=True,
             )
 
-        def gate_tanh(u, cols, ga):
-            nc.scalar.activation(tanh[:, cols], ga, ACT.Tanh, bias=half_bias[:, u : u + 1], scale=0.5)
-
-        def transform(u, parts, ha):
+        def transform(u, parts, ha, names):
             for part, (codes, plane) in enumerate(parts):
                 nc.tensor.matmul_mx(
                     out=ha,
@@ -149,41 +145,39 @@ def tile_list_hwayt_hl_gelu_kernel(
                     start=(part == 0),
                     stop=(part == 1),
                 )
-            for cols in halves:
-                nc.scalar.activation(gelus[u][:, cols], ha[:, cols], ACT.Gelu_apprx_tanh, bias=gelu_bias[:])
+            gelus = [sb.tile([P, HALF], F32, name=name, align_bytes=64) for name in names]
+            for cols, gelu in zip(halves, gelus):
+                nc.scalar.activation(gelu[:], ha[:, cols], ACT.Gelu_apprx_tanh, bias=gelu_bias[:])
+            return gelus
 
-        for cols, bank in ((slice(0, P), "bank0"), (slice(P, HALF), "bank2"), (halves[1], "bank1")):
-            ga_part = ps.tile([P, cols.stop - cols.start], F32, name=bank)[:]
-            gate_sum(1, cols, ga_part)
-            gate_tanh(1, cols, ga_part)
-            if cols.stop % HALF == 0:
-                done = slice(cols.stop - HALF, cols.stop)
-                nc.scalar.activation(keep[:, done], tanh[:, done], ACT.Identity, bias=0.5, scale=-0.5)
+        for h, cols in enumerate(halves):
+            tanh = per_row_tile("tanh", [P, HALF], F32)
+            for u in (1, 0):
+                ga = ps.tile([P, HALF], F32, name="bank%d" % (2 * h + 1 - u))[:]
+                gate_sum(u, cols, ga)
+                nc.scalar.activation(tanh[u][:], ga, ACT.Tanh, bias=half_bias[:, u : u + 1], scale=0.5)
+            for u in (1, 0):
+                nc.scalar.activation(keep[u][:, cols], tanh[u][:], ACT.Identity, bias=0.5, scale=-0.5)
         quantise(codes0[:], plane0[:], staging[:])
-        transform(0, [(codes0[:, c], plane0[:, c]) for c in (slice(0, P), slice(P, 2 * P))], ps.tile([P, J], F32, name="bank0")[:])
+        parts0 = [(codes0[:, c], plane0[:, c]) for c in (slice(0, P), slice(P, 2 * P))]
+        gelus = [transform(0, parts0, ps.tile([P, J], F32, name="bank0")[:], ("tanh1", "tanh0"))]
         nc.vector.tensor_tensor(
             words_by_pairs(by_word(lo1[:])), rows_by_pairs(w_raw[1][:]), words_by_pairs(by_word(hi1[:])), ALU.subtract
         )
         quantise(codes1[0][:], plane1[0], hi1[:])
         quantise(codes1[1][:], plane1[1], lo1[:])
-        transform(1, [(codes1[part][:], plane1[part]) for part in range(2)], ps.tile([P, J], F32, name="bank1")[:])
-        ga0 = ps.tile([P, J], F32, name="bank0")
-        gate_sum(0, slice(0, J), ga0[:])
-        gate_tanh(0, slice(0, J), ga0[:])
+        parts1 = [(codes1[part][:], plane1[part]) for part in range(2)]
+        gelus.append(transform(1, parts1, ps.tile([P, J], F32, name="bank2")[:], ("gelu1a", "gelu1b")))
 
-        carried = sb.tile([P, J], F32, name="w_raw1", align_bytes=64)
+        carried = [sb.tile([P, J], F32, name="w_raw%d" % u, align_bytes=64) for u in range(ROW_TILES)]
         for cols in halves:
-            nc.vector.tensor_tensor(carried[:, cols], r_rows[1][:].indirect(listed(cols)), keep[:, cols], ALU.mult)
-        for cols in halves:
-            nc.vector.tensor_tensor(diff[:, cols], r_rows[0][:].indirect(listed(cols)), gelus[0][:, cols], ALU.subtract)
-        made = sb.tile([P, J], F32, name="made", align_bytes=64)
-        for cols in halves:
-            nc.vector.scalar_tensor_tensor(made[:, cols], keep[:, cols], 1.0, gelus[1][:, cols], ALU.subtract, ALU.mult)
-        for cols in halves:
-            nc.vector.tensor_tensor(result[1][:, cols], carried[:, cols], made[:, cols], ALU.subtract)
-            nc.sync.dma_start(out=out[P : 2 * P, cols], in_=result[1][:, cols])
-        for cols in halves:
-            nc.vector.scalar_tensor_tensor(scaled[:, cols], tanh[:, cols], 1.0, diff[:, cols], ALU.subtract, ALU.mult)
-        for cols in halves:
-            nc.vector.scalar_tensor_tensor(result[0][:, cols], scaled[:, cols], -0.5, gelus[0][:, cols], ALU.mult, ALU.add)
-            nc.sync.dma_start(out=out[0:P, cols], in_=result[0][:, cols])
+            for u in (1, 0):
+                nc.vector.tensor_tensor(carried[u][:, cols], r_rows[u][:].indirect(listed(cols)), keep[u][:, cols], ALU.mult)
+        for u in range(ROW_TILES):
+            for cols, gelu in zip(halves, gelus[u]):
+                nc.vector.scalar_tensor_tensor(
+                    made[u][:, cols], keep[u][:, cols], 1.0, gelu[:], ALU.subtract, ALU.mult
+                )
+            for cols in halves:
+                nc.vector.tensor_tensor(result[u][:, cols], carried[u][:, cols], made[u][:, cols], ALU.subtract)
+                nc.sync.dma_start(out=out[u * P : (u + 1) * P, cols], in_=result[u][:, cols])

@@ -52,13 +52,13 @@ def tile_list_hwayt_hl_gelu_kernel(
         w_raw = [sb.tile([P, PACK, P], F32, name="w_raw%d" % u, align_bytes=64) for u in range(ROW_TILES)]
         r_rows = [sb.tile([P, T], F32, name="r_rows%d" % u, align_bytes=64) for u in range(ROW_TILES)]
 
-        nc.gpsimd.memset(tab_plane[:].bitcast(I32), 0)
+        nc.vector.memset(tab_plane[:].bitcast(I32), 0)
         nc.gpsimd.memset(zero[:], 0.0)
         nc.vector.memset(wg_plane[:].bitcast(I32), 0)
 
         nc.gpsimd.dma_start(out=wg_codes[:].bitcast(I32), in_=wg_words[0].bitcast(I32))
         w_rows = wh.rearrange("(p i) n -> p i n", i=PACK)
-        nc.scalar.dma_start(out=w_raw[0][:], in_=w_rows[:, :, 0:P])
+        nc.sync.dma_start(out=w_raw[0][:], in_=w_rows[:, :, 0:P])
         nc.sync.dma_start(offsets[:], offs)
         load_scale_rows([nc.sync], tab_plane, tab_scales[0])
         nc.scalar.activation(gelu_bias[:], zero[:], ACT.Gelu_apprx_tanh)
@@ -99,8 +99,6 @@ def tile_list_hwayt_hl_gelu_kernel(
         def quantise(codes, plane, values):
             nc.vector.quantize_mx(out=codes.bitcast(FP8X4), scales=plane, in_=values)
 
-        nc.vector.tensor_copy(v_plane[:, halves[0]], tab_plane[:].indirect(listed(halves[0])))
-
         def rows_by_pairs(ap):
             return ap.rearrange("p i (c e) -> p c i e", e=2)
 
@@ -115,7 +113,7 @@ def tile_list_hwayt_hl_gelu_kernel(
         word_halves = w_raw[1][:].bitcast(BF16).rearrange("p i (n h) -> p i n h", h=2)
         nc.scalar.copy(words_by_pairs(upper[:]), rows_by_pairs(word_halves[:, :, :, 1]))
         nc.scalar.mul(half_bias[:], bias[:], 0.5)
-        nc.vector.tensor_copy(v_plane[:, halves[1]], tab_plane[:].indirect(listed(halves[1])))
+        nc.vector.tensor_copy(v_plane[:], tab_plane[:].indirect(offsets[:]))
         for cols in halves:
             nc.vector.tensor_copy(v_codes[:, cols], tab_codes[:].indirect(listed(cols)))
         hi1 = sb.tile([P, WOVEN], BF16, name="hi32", align_bytes=64)

@@ -19,17 +19,16 @@ ACT = mybir.ActivationFunctionType
 P = 128
 PACK = 4
 ROW_TILES = N // P
-WOVEN = P * PACK
 HALF = J // 2
-LONG = 320
+RUN = 2
 HI_MASK = 0xFFF00000 - (1 << 32)
 HI_MASK_PAIR = 0xFFF0FFF0 - (1 << 32)
 
 
-def load_scale_rows(queues, plane, rows):
+def load_scale_rows(nc, plane, rows):
     words = rows.bitcast(I32)
     for q in range(4):
-        queues[q % len(queues)].dma_start(out=plane[32 * q : 32 * q + 4, :].bitcast(I32), in_=words[4 * q : 4 * q + 4, :])
+        nc.sync.dma_start(out=plane[32 * q : 32 * q + 4, :].bitcast(I32), in_=words[4 * q : 4 * q + 4, :])
 
 
 def tile_list_hwayt_hl_gelu_kernel(
@@ -40,17 +39,23 @@ def tile_list_hwayt_hl_gelu_kernel(
         sb = ctx.enter_context(tc.tile_pool(name="sb", bufs=1))
         ps = ctx.enter_context(tc.psum_pool(name="ps", bufs=1))
 
+        def tile(name, shape, dtype):
+            return sb.tile(shape, dtype, name=name, align_bytes=64)
+
+        def per_row_tile(name, shape, dtype):
+            return [tile("%s%d" % (name, u), shape, dtype) for u in range(ROW_TILES)]
+
         offsets = sb.tile([P, J // 16], U16, name="offsets")
-        tab_plane = sb.tile([P, T], U8, name="tab_plane", align_bytes=64)
-        tab_codes = sb.tile([P, T], U32, name="tab_codes", align_bytes=64)
-        wg_plane = sb.tile([P, N], U8, name="wg_plane", align_bytes=64)
-        wg_codes = sb.tile([P, 2 * N], U8, name="wg_codes", align_bytes=64)
-        bias = sb.tile([P, ROW_TILES], F32, name="bias")
-        half_bias = sb.tile([P, ROW_TILES], F32, name="half_bias")
-        zero = sb.tile([P, 1], F32, name="zero")
-        gelu_bias = sb.tile([P, 1], F32, name="gelu_bias")
-        w_raw = [sb.tile([P, PACK, P], F32, name="w_raw%d" % u, align_bytes=64) for u in range(ROW_TILES)]
-        r_rows = [sb.tile([P, T], F32, name="r_rows%d" % u, align_bytes=64) for u in range(ROW_TILES)]
+        tab_plane = tile("tab_plane", [P, T], U8)
+        tab_codes = tile("tab_codes", [P, T], U32)
+        wg_plane = tile("wg_plane", [P, N], U8)
+        wg_codes = tile("wg_codes", [P, 2 * N], U8)
+        bias = tile("bias", [P, ROW_TILES], F32)
+        half_bias = tile("half_bias", [P, ROW_TILES], F32)
+        zero = tile("zero", [P, 1], F32)
+        gelu_bias = tile("gelu_bias", [P, 1], F32)
+        w_raw = per_row_tile("w_raw", [P, PACK, P], F32)
+        r_rows = per_row_tile("r_rows", [P, T], F32)
 
         nc.vector.memset(tab_plane[:].bitcast(I32), 0)
         nc.gpsimd.memset(zero[:], 0.0)
@@ -60,35 +65,20 @@ def tile_list_hwayt_hl_gelu_kernel(
         w_rows = wh.rearrange("(p i) n -> p i n", i=PACK)
         nc.sync.dma_start(out=w_raw[0][:], in_=w_rows[:, :, 0:P])
         nc.sync.dma_start(offsets[:], offs)
-        load_scale_rows([nc.sync], tab_plane, tab_scales[0])
+        load_scale_rows(nc, tab_plane, tab_scales[0])
         nc.scalar.activation(gelu_bias[:], zero[:], ACT.Gelu_apprx_tanh)
         nc.sync.dma_start(out=tab_codes[:].bitcast(I32), in_=tab_words[0].rearrange("p t i -> p (t i)").bitcast(I32))
         nc.sync.dma_start(out=w_raw[1][:], in_=w_rows[:, :, P : 2 * P])
-        load_scale_rows([nc.sync], wg_plane, wg_scales[0])
+        load_scale_rows(nc, wg_plane, wg_scales[0])
         with nc.allow_non_contiguous_dma(reason="one bias value a partition"):
             nc.sync.dma_start(out=bias[:], in_=bg.rearrange("(u p) -> p u", p=P))
-        nc.sync.dma_start(out=r_rows[1][:], in_=rT[P : 2 * P, :])
-        nc.sync.dma_start(out=r_rows[0][:], in_=rT[0:P, :])
+        for u in range(ROW_TILES):
+            nc.sync.dma_start(out=r_rows[u][:], in_=rT[u * P : (u + 1) * P, :])
 
-        def per_row_tile(name, shape, dtype):
-            return [sb.tile(shape, dtype, name="%s%d" % (name, u), align_bytes=64) for u in range(ROW_TILES)]
-
-        hi32 = sb.tile([P, P, PACK], F32, name="hi32", align_bytes=64)
-        upper = sb.tile([P, P, PACK], BF16, name="upper", align_bytes=64)
-        staging = sb.tile([P, 2 * WOVEN], BF16, name="staging", align_bytes=64)
-        lo1 = sb.tile([P, WOVEN], BF16, name="lo1", align_bytes=64)
-        codes0 = sb.tile([P, 2 * P], U32, name="codes0", align_bytes=64)
-        plane0 = sb.tile([P, 2 * P], U8, name="plane0", align_bytes=64)
-        codes1 = [sb.tile([P, P], U32, name="codes1_%d" % part, align_bytes=64) for part in range(2)]
-        plane1 = [sb.tile([P, P], U8, name="plane1_%d" % part, align_bytes=64)[:] for part in range(2)]
-        result = per_row_tile("result", [P, J], F32)
-        keep = per_row_tile("keep", [P, J], F32)
-        made = per_row_tile("made", [P, J], F32)
-        v_plane = sb.tile([P, J], U8, name="v_plane", align_bytes=64)
-        v_codes = sb.tile([P, J], U32, name="v_codes", align_bytes=64)
-        woven = [w_raw[u][:].rearrange("p i n -> p n i") for u in range(ROW_TILES)]
+        WOVEN = P * PACK
         halves = [slice(0, HALF), slice(HALF, J)]
-        ends = [slice(0, LONG), slice(LONG, J)]
+        first, second = halves
+        ends = [slice(HALF, HALF + P), slice(HALF + P, J)]
 
         def listed(cols):
             return offsets[:, cols.start // 16 : cols.stop // 16]
@@ -96,34 +86,48 @@ def tile_list_hwayt_hl_gelu_kernel(
         def by_word(ap):
             return ap.rearrange("p (n i) -> p n i", i=PACK)
 
+        def rows_in_runs(ap):
+            return ap.rearrange("p i (c e) -> p c i e", e=RUN)
+
+        def words_in_runs(ap):
+            return ap.rearrange("p (c e i) -> p c i e", e=RUN, i=PACK)
+
         def quantise(codes, plane, values):
             nc.vector.quantize_mx(out=codes.bitcast(FP8X4), scales=plane, in_=values)
 
-        def rows_by_pairs(ap):
-            return ap.rearrange("p i (c e) -> p c i e", e=2)
-
-        def words_by_pairs(ap):
-            return ap.rearrange("p (c e) i -> p c i e", e=2)
+        hi32 = tile("hi32", [P, WOVEN], F32)
+        upper = tile("upper", [P, WOVEN], BF16)
+        staging = tile("staging", [P, 2 * WOVEN], BF16)
+        lo1 = tile("lo1", [P, WOVEN], BF16)
+        codes0 = tile("codes0", [P, 2 * P], U32)
+        plane0 = tile("plane0", [P, 2 * P], U8)
+        codes1 = [tile("codes1_%d" % part, [P, P], U32) for part in range(2)]
+        plane1 = [tile("plane1_%d" % part, [P, P], U8) for part in range(2)]
+        v_plane = tile("v_plane", [P, J], U8)
+        v_codes = tile("v_codes", [P, J], U32)
 
         nc.vector.tensor_single_scalar(
-            words_by_pairs(hi32[:].bitcast(I32)), rows_by_pairs(w_raw[0][:].bitcast(I32)), HI_MASK, ALU.bitwise_and
+            words_in_runs(hi32[:].bitcast(I32)), rows_in_runs(w_raw[0][:].bitcast(I32)), HI_MASK, ALU.bitwise_and
         )
-        nc.gpsimd.tensor_tensor(by_word(staging[:, WOVEN:]), woven[0], hi32[:], ALU.subtract)
-        nc.scalar.copy(staging[:, :WOVEN], hi32[:].rearrange("p n i -> p (n i)"))
+        nc.gpsimd.tensor_tensor(
+            by_word(staging[:, WOVEN:]), w_raw[0][:].rearrange("p i n -> p n i"), by_word(hi32[:]), ALU.subtract
+        )
+        nc.scalar.copy(staging[:, :WOVEN], hi32[:])
         word_halves = w_raw[1][:].bitcast(BF16).rearrange("p i (n h) -> p i n h", h=2)
-        nc.scalar.copy(words_by_pairs(upper[:]), rows_by_pairs(word_halves[:, :, :, 1]))
+        nc.scalar.copy(words_in_runs(upper[:]), rows_in_runs(word_halves[:, :, :, 1]))
         nc.scalar.mul(half_bias[:], bias[:], 0.5)
         nc.vector.tensor_copy(v_plane[:], tab_plane[:].indirect(offsets[:]))
         for cols in halves:
             nc.vector.tensor_copy(v_codes[:, cols], tab_codes[:].indirect(listed(cols)))
-        hi1 = sb.tile([P, WOVEN], BF16, name="hi32", align_bytes=64)
-        nc.vector.tensor_single_scalar(
-            hi1[:].bitcast(I32), upper[:].rearrange("p n i -> p (n i)").bitcast(I32), HI_MASK_PAIR, ALU.bitwise_and
-        )
+        hi1 = tile("hi32", [P, WOVEN], BF16)
+        nc.vector.tensor_single_scalar(hi1[:].bitcast(I32), upper[:].bitcast(I32), HI_MASK_PAIR, ALU.bitwise_and)
 
-        def gate_sum(u, cols, ga):
+        keep = per_row_tile("keep", [P, J], F32)
+
+        def gate_tanh(u, cols, bank, name):
+            ga = ps.tile([P, HALF], F32, name=bank)
             nc.tensor.matmul_mx(
-                out=ga,
+                out=ga[:],
                 lhsT=wg_codes[:, 2 * u * P : 2 * (u + 1) * P].bitcast(FP4X4),
                 lhsT_scale=wg_plane[:, u * P : (u + 1) * P],
                 rhs=v_codes[:, cols].bitcast(FP8X4),
@@ -131,11 +135,18 @@ def tile_list_hwayt_hl_gelu_kernel(
                 start=True,
                 stop=True,
             )
+            tanh = tile(name, [P, HALF], F32)
+            nc.scalar.activation(tanh[:], ga[:], ACT.Tanh, bias=half_bias[:, u : u + 1], scale=0.5)
+            return tanh
 
-        def transform(u, parts, ha, names):
+        def keep_of(u, cols, tanh):
+            nc.scalar.activation(keep[u][:, cols], tanh[:], ACT.Identity, bias=0.5, scale=-0.5)
+
+        def transform(parts, bank):
+            ha = ps.tile([P, J], F32, name=bank)
             for part, (codes, plane) in enumerate(parts):
                 nc.tensor.matmul_mx(
-                    out=ha,
+                    out=ha[:],
                     lhsT=codes.bitcast(FP8X4),
                     lhsT_scale=plane,
                     rhs=v_codes[:].bitcast(FP8X4),
@@ -143,39 +154,61 @@ def tile_list_hwayt_hl_gelu_kernel(
                     start=(part == 0),
                     stop=(part == 1),
                 )
-            gelus = [sb.tile([P, HALF], F32, name=name, align_bytes=64) for name in names]
-            for cols, gelu in zip(halves, gelus):
-                nc.scalar.activation(gelu[:], ha[:, cols], ACT.Gelu_apprx_tanh, bias=gelu_bias[:])
-            return gelus
+            return ha
 
-        for h, cols in enumerate(halves):
-            tanh = per_row_tile("tanh", [P, HALF], F32)
-            for u in (1, 0):
-                ga = ps.tile([P, HALF], F32, name="bank%d" % (2 * h + 1 - u))[:]
-                gate_sum(u, cols, ga)
-                nc.scalar.activation(tanh[u][:], ga, ACT.Tanh, bias=half_bias[:, u : u + 1], scale=0.5)
-            for u in (1, 0):
-                nc.scalar.activation(keep[u][:, cols], tanh[u][:], ACT.Identity, bias=0.5, scale=-0.5)
+        def gelu_of(ha, cols, name):
+            gelu = tile(name, [P, HALF], F32)
+            nc.scalar.activation(gelu[:], ha[:, cols], ACT.Gelu_apprx_tanh, bias=gelu_bias[:])
+            return gelu
+
+        def carry(u, cols, into):
+            nc.vector.tensor_tensor(into, r_rows[u][:].indirect(listed(cols)), keep[u][:, cols], ALU.mult)
+
+        result = per_row_tile("result", [P, J], F32)
+
+        def make(u, cols, gelu):
+            made = tile("made%d%d" % (u, cols.start // HALF), [P, HALF], F32)
+            nc.vector.scalar_tensor_tensor(made[:], keep[u][:, cols], 1.0, gelu[:], ALU.subtract, ALU.mult)
+            return made
+
+        def finish(u, cols, carried, made):
+            nc.vector.tensor_tensor(result[u][:, cols], carried, made, ALU.subtract)
+            nc.sync.dma_start(out=out[u * P : (u + 1) * P, cols], in_=result[u][:, cols])
+
+        tanh0a = gate_tanh(0, first, "bank0", "tanh0a")
+        tanh1a = gate_tanh(1, first, "bank1", "tanh1a")
+        keep_of(0, first, tanh0a)
+        keep_of(1, first, tanh1a)
+        tanh0b = gate_tanh(0, second, "bank2", "tanh0a")
+        tanh1b = gate_tanh(1, second, "bank3", "tanh1a")
+        keep_of(0, second, tanh0b)
+        keep_of(1, second, tanh1b)
+
         quantise(codes0[:], plane0[:], staging[:])
-        parts0 = [(codes0[:, c], plane0[:, c]) for c in (slice(0, P), slice(P, 2 * P))]
-        gelus = [transform(0, parts0, ps.tile([P, J], F32, name="bank0")[:], ("tanh1", "tanh0"))]
-        nc.vector.tensor_tensor(
-            words_by_pairs(by_word(lo1[:])), rows_by_pairs(w_raw[1][:]), words_by_pairs(by_word(hi1[:])), ALU.subtract
-        )
-        quantise(codes1[0][:], plane1[0], hi1[:])
-        quantise(codes1[1][:], plane1[1], lo1[:])
-        parts1 = [(codes1[part][:], plane1[part]) for part in range(2)]
-        gelus.append(transform(1, parts1, ps.tile([P, J], F32, name="bank2")[:], ("gelu1a", "gelu1b")))
+        ha0 = transform([(codes0[:, c], plane0[:, c]) for c in (slice(0, P), slice(P, 2 * P))], "bank0")
+        gelu0 = [gelu_of(ha0, first, "tanh0a"), gelu_of(ha0, second, "tanh1a")]
+        nc.vector.tensor_tensor(words_in_runs(lo1[:]), rows_in_runs(w_raw[1][:]), words_in_runs(hi1[:]), ALU.subtract)
+        quantise(codes1[0][:], plane1[0][:], hi1[:])
+        quantise(codes1[1][:], plane1[1][:], lo1[:])
+        ha1 = transform([(codes1[part][:], plane1[part][:]) for part in range(2)], "bank2")
 
-        carried = [sb.tile([P, J], F32, name="w_raw%d" % u, align_bytes=64) for u in range(ROW_TILES)]
-        for cols in halves:
-            for u in (1, 0):
-                nc.vector.tensor_tensor(carried[u][:, cols], r_rows[u][:].indirect(listed(cols)), keep[u][:, cols], ALU.mult)
-        for u in range(ROW_TILES):
-            for cols, gelu in zip(halves, gelus[u]):
-                nc.vector.scalar_tensor_tensor(
-                    made[u][:, cols], keep[u][:, cols], 1.0, gelu[:], ALU.subtract, ALU.mult
-                )
-            for cols in halves:
-                nc.vector.tensor_tensor(result[u][:, cols], carried[u][:, cols], made[u][:, cols], ALU.subtract)
-                nc.sync.dma_start(out=out[u * P : (u + 1) * P, cols], in_=result[u][:, cols])
+        carried0 = tile("w_raw1", [P, J], F32)
+        carried1a = tile("w_raw0", [P, HALF], F32)
+        carry(0, first, carried0[:, first])
+        carry(1, first, carried1a[:])
+        carry(0, second, carried0[:, second])
+        made0 = [make(0, cols, gelu) for cols, gelu in zip(halves, gelu0)]
+        for cols, made in zip(halves, made0):
+            finish(0, cols, carried0[:, cols], made[:])
+
+        gelu1a = gelu_of(ha1, first, "gelu1a")
+        gelu1b = gelu_of(ha1, second, "gelu1b")
+        made1a = make(1, first, gelu1a)
+        made1b = make(1, second, gelu1b)
+        finish(1, first, carried1a[:], made1a[:])
+        carried1b = tile("gelu1a", [P, HALF], F32)
+        for cols in ends:
+            carry(1, cols, carried1b[:, cols.start - HALF : cols.stop - HALF])
+        for cols in ends:
+            part = slice(cols.start - HALF, cols.stop - HALF)
+            finish(1, cols, carried1b[:, part], made1b[:, part])

@@ -83,19 +83,16 @@ def tile_list_hwayt_hl_gelu_kernel(
         def listed(cols):
             return offsets[:, cols.start // 16 : cols.stop // 16]
 
-        def by_word(ap):
-            return ap.rearrange("p (n i) -> p n i", i=PACK)
+        def rows_in_runs(ap, run=RUN):
+            return ap.rearrange("p i (c e) -> p c i e", e=run)
 
-        def rows_in_runs(ap):
-            return ap.rearrange("p i (c e) -> p c i e", e=RUN)
-
-        def words_in_runs(ap):
-            return ap.rearrange("p (c e i) -> p c i e", e=RUN, i=PACK)
+        def words_in_runs(ap, run=RUN):
+            return ap.rearrange("p (c e i) -> p c i e", e=run, i=PACK)
 
         def quantise(codes, plane, values):
             nc.vector.quantize_mx(out=codes.bitcast(FP8X4), scales=plane, in_=values)
 
-        hi32 = tile("hi32", [P, WOVEN], F32)
+        hi32 = tile("hi32", [P, PACK, P], F32)
         upper = tile("upper", [P, WOVEN], BF16)
         staging = tile("staging", [P, 2 * WOVEN], BF16)
         lo1 = tile("lo1", [P, WOVEN], BF16)
@@ -106,13 +103,11 @@ def tile_list_hwayt_hl_gelu_kernel(
         v_plane = tile("v_plane", [P, J], U8)
         v_codes = tile("v_codes", [P, J], U32)
 
-        nc.vector.tensor_single_scalar(
-            words_in_runs(hi32[:].bitcast(I32)), rows_in_runs(w_raw[0][:].bitcast(I32)), HI_MASK, ALU.bitwise_and
-        )
+        nc.vector.tensor_single_scalar(hi32[:].bitcast(I32), w_raw[0][:].bitcast(I32), HI_MASK, ALU.bitwise_and)
         nc.gpsimd.tensor_tensor(
-            by_word(staging[:, WOVEN:]), w_raw[0][:].rearrange("p i n -> p n i"), by_word(hi32[:]), ALU.subtract
+            words_in_runs(staging[:, WOVEN:], 4), rows_in_runs(w_raw[0][:], 4), rows_in_runs(hi32[:], 4), ALU.subtract
         )
-        nc.scalar.copy(staging[:, :WOVEN], hi32[:])
+        nc.scalar.copy(words_in_runs(staging[:, :WOVEN]), rows_in_runs(hi32[:]))
         word_halves = w_raw[1][:].bitcast(BF16).rearrange("p i (n h) -> p i n h", h=2)
         nc.scalar.copy(words_in_runs(upper[:]), rows_in_runs(word_halves[:, :, :, 1]))
         nc.scalar.mul(half_bias[:], bias[:], 0.5)
@@ -122,7 +117,7 @@ def tile_list_hwayt_hl_gelu_kernel(
         hi1 = tile("hi32", [P, WOVEN], BF16)
         nc.vector.tensor_single_scalar(hi1[:].bitcast(I32), upper[:].bitcast(I32), HI_MASK_PAIR, ALU.bitwise_and)
 
-        keep = per_row_tile("keep", [P, J], F32)
+        keep = {}
 
         def gate_tanh(u, cols, bank, name):
             ga = ps.tile([P, HALF], F32, name=bank)
@@ -139,8 +134,14 @@ def tile_list_hwayt_hl_gelu_kernel(
             nc.scalar.activation(tanh[:], ga[:], ACT.Tanh, bias=half_bias[:, u : u + 1], scale=0.5)
             return tanh
 
-        def keep_of(u, cols, tanh):
-            nc.scalar.activation(keep[u][:, cols], tanh[:], ACT.Identity, bias=0.5, scale=-0.5)
+        def keep_of(u, cols, tanh, name=None):
+            half = cols.start // HALF
+            keep[u, half] = tile(name or "keep%d%d" % (u, half), [P, HALF], F32)
+            nc.scalar.activation(keep[u, half][:], tanh[:], ACT.Identity, bias=0.5, scale=-0.5)
+
+        def kept(u, cols):
+            half = cols.start // HALF
+            return keep[u, half][:, cols.start - half * HALF : cols.stop - half * HALF]
 
         def transform(parts, bank):
             ha = ps.tile([P, J], F32, name=bank)
@@ -156,19 +157,18 @@ def tile_list_hwayt_hl_gelu_kernel(
                 )
             return ha
 
-        def gelu_of(ha, cols, name):
-            gelu = tile(name, [P, HALF], F32)
-            nc.scalar.activation(gelu[:], ha[:, cols], ACT.Gelu_apprx_tanh, bias=gelu_bias[:])
+        def gelu_of(ha, cols, gelu):
+            nc.scalar.activation(gelu, ha[:, cols], ACT.Gelu_apprx_tanh, bias=gelu_bias[:])
             return gelu
 
         def carry(u, cols, into):
-            nc.vector.tensor_tensor(into, r_rows[u][:].indirect(listed(cols)), keep[u][:, cols], ALU.mult)
+            nc.vector.tensor_tensor(into, r_rows[u][:].indirect(listed(cols)), kept(u, cols), ALU.mult)
 
         result = per_row_tile("result", [P, J], F32)
 
         def make(u, cols, gelu):
             made = tile("made%d%d" % (u, cols.start // HALF), [P, HALF], F32)
-            nc.vector.scalar_tensor_tensor(made[:], keep[u][:, cols], 1.0, gelu[:], ALU.subtract, ALU.mult)
+            nc.vector.scalar_tensor_tensor(made[:], kept(u, cols), 1.0, gelu, ALU.subtract, ALU.mult)
             return made
 
         def finish(u, cols, carried, made):
@@ -182,11 +182,11 @@ def tile_list_hwayt_hl_gelu_kernel(
         tanh0b = gate_tanh(0, second, "bank2", "tanh0a")
         tanh1b = gate_tanh(1, second, "bank3", "tanh1a")
         keep_of(0, second, tanh0b)
-        keep_of(1, second, tanh1b)
 
         quantise(codes0[:], plane0[:], staging[:])
         ha0 = transform([(codes0[:, c], plane0[:, c]) for c in (slice(0, P), slice(P, 2 * P))], "bank0")
-        gelu0 = [gelu_of(ha0, first, "tanh0a"), gelu_of(ha0, second, "tanh1a")]
+        both = tile("tanh0a", [P, J], F32)
+        gelu0 = [gelu_of(ha0, cols, both[:, cols]) for cols in halves]
         nc.vector.tensor_tensor(words_in_runs(lo1[:]), rows_in_runs(w_raw[1][:]), words_in_runs(hi1[:]), ALU.subtract)
         quantise(codes1[0][:], plane1[0][:], hi1[:])
         quantise(codes1[1][:], plane1[1][:], lo1[:])
@@ -201,8 +201,9 @@ def tile_list_hwayt_hl_gelu_kernel(
         for cols, made in zip(halves, made0):
             finish(0, cols, carried0[:, cols], made[:])
 
-        gelu1a = gelu_of(ha1, first, "gelu1a")
-        gelu1b = gelu_of(ha1, second, "gelu1b")
+        keep_of(1, second, tanh1b, "tanh0a")
+        gelu1a = gelu_of(ha1, first, tile("gelu1a", [P, HALF], F32)[:])
+        gelu1b = gelu_of(ha1, second, tile("gelu1b", [P, HALF], F32)[:])
         made1a = make(1, first, gelu1a)
         made1b = make(1, second, gelu1b)
         finish(1, first, carried1a[:], made1a[:])

from contextlib import ExitStack

import concourse.mybir as mybir

K, N, T, J = 512, 256, 1024, 512
FLOPS = 3 * 2 * K * N * J

F32 = mybir.dt.float32
BF16 = mybir.dt.bfloat16
I32 = mybir.dt.int32
U32 = mybir.dt.uint32
U16 = mybir.dt.uint16
U8 = mybir.dt.uint8
FP8X4 = mybir.dt.float8_e4m3fn_x4
FP4X4 = mybir.dt.float4_e2m1fn_x4
ALU = mybir.AluOpType
ACT = mybir.ActivationFunctionType

P = 128
PACK = 4
ROW_TILES = N // P
HALF = J // 2
RUN = 2
HI_MASK = 0xFFF00000 - (1 << 32)
HI_MASK_PAIR = 0xFFF0FFF0 - (1 << 32)


def load_scale_rows(nc, plane, rows):
    words = rows.bitcast(I32)
    for q in range(4):
        nc.sync.dma_start(out=plane[32 * q : 32 * q + 4, :].bitcast(I32), in_=words[4 * q : 4 * q + 4, :])


def tile_list_hwayt_hl_gelu_kernel(
    tc, tab_words, tab_scales, wg_words, wg_scales, wh, bg, rT, offs, out
):
    nc = tc.nc
    with ExitStack() as ctx:
        sb = ctx.enter_context(tc.tile_pool(name="sb", bufs=1))
        ps = ctx.enter_context(tc.psum_pool(name="ps", bufs=1))

        def tile(name, shape, dtype):
            return sb.tile(shape, dtype, name=name, align_bytes=64)

        def per_row_tile(name, shape, dtype):
            return [tile("%s%d" % (name, u), shape, dtype) for u in range(ROW_TILES)]

        offsets = sb.tile([P, J // 16], U16, name="offsets")
        tab_plane = tile("tab_plane", [P, T], U8)
        tab_codes = tile("tab_codes", [P, T], U32)
        wg_plane = tile("wg_plane", [P, N], U8)
        wg_codes = tile("wg_codes", [P, 2 * N], U8)
        bias = tile("bias", [P, ROW_TILES], F32)
        half_bias = tile("half_bias", [P, ROW_TILES], F32)
        zero = tile("zero", [P, 1], F32)
        gelu_bias = tile("gelu_bias", [P, 1], F32)
        w_raw = per_row_tile("w_raw", [P, PACK, P], F32)
        r_rows = per_row_tile("r_rows", [P, T], F32)

        nc.vector.memset(tab_plane[:].bitcast(I32), 0)
        nc.gpsimd.memset(zero[:], 0.0)
        nc.vector.memset(wg_plane[:].bitcast(I32), 0)

        nc.gpsimd.dma_start(out=wg_codes[:].bitcast(I32), in_=wg_words[0].bitcast(I32))
        w_rows = wh.rearrange("(p i) n -> p i n", i=PACK)
        nc.sync.dma_start(out=w_raw[0][:], in_=w_rows[:, :, 0:P])
        nc.sync.dma_start(offsets[:], offs)
        load_scale_rows(nc, tab_plane, tab_scales[0])
        nc.scalar.activation(gelu_bias[:], zero[:], ACT.Gelu_apprx_tanh)
        nc.sync.dma_start(out=tab_codes[:].bitcast(I32), in_=tab_words[0].rearrange("p t i -> p (t i)").bitcast(I32))
        nc.sync.dma_start(out=w_raw[1][:], in_=w_rows[:, :, P : 2 * P])
        load_scale_rows(nc, wg_plane, wg_scales[0])
        with nc.allow_non_contiguous_dma(reason="one bias value a partition"):
            nc.sync.dma_start(out=bias[:], in_=bg.rearrange("(u p) -> p u", p=P))
        for u in range(ROW_TILES):
            nc.sync.dma_start(out=r_rows[u][:], in_=rT[u * P : (u + 1) * P, :])

        WOVEN = P * PACK
        halves = [slice(0, HALF), slice(HALF, J)]
        first, second = halves
        ends = [slice(HALF, HALF + P), slice(HALF + P, J)]

        def listed(cols):
            return offsets[:, cols.start // 16 : cols.stop // 16]

        def rows_in_runs(ap, run=RUN):
            return ap.rearrange("p i (c e) -> p c i e", e=run)

        def words_in_runs(ap, run=RUN):
            return ap.rearrange("p (c e i) -> p c i e", e=run, i=PACK)

        def quantise(codes, plane, values):
            nc.vector.quantize_mx(out=codes.bitcast(FP8X4), scales=plane, in_=values)

        hi32 = tile("hi32", [P, PACK, P], F32)
        upper = tile("upper", [P, WOVEN], BF16)
        staging = tile("staging", [P, 2 * WOVEN], BF16)
        lo1 = tile("lo1", [P, WOVEN], BF16)
        codes0 = tile("codes0", [P, 2 * P], U32)
        plane0 = tile("plane0", [P, 2 * P], U8)
        codes1 = [tile("codes1_%d" % part, [P, P], U32) for part in range(2)]
        plane1 = [tile("plane1_%d" % part, [P, P], U8) for part in range(2)]
        v_plane = tile("v_plane", [P, J], U8)
        v_codes = tile("v_codes", [P, J], U32)

        nc.vector.tensor_single_scalar(hi32[:].bitcast(I32), w_raw[0][:].bitcast(I32), HI_MASK, ALU.bitwise_and)
        nc.gpsimd.tensor_tensor(
            words_in_runs(staging[:, WOVEN:], 4), rows_in_runs(w_raw[0][:], 4), rows_in_runs(hi32[:], 4), ALU.subtract
        )
        nc.scalar.copy(words_in_runs(staging[:, :WOVEN]), rows_in_runs(hi32[:]))
        word_halves = w_raw[1][:].bitcast(BF16).rearrange("p i (n h) -> p i n h", h=2)
        nc.scalar.copy(words_in_runs(upper[:]), rows_in_runs(word_halves[:, :, :, 1]))
        nc.scalar.mul(half_bias[:], bias[:], 0.5)
        nc.vector.tensor_copy(v_plane[:], tab_plane[:].indirect(offsets[:]))
        for cols in halves:
            nc.vector.tensor_copy(v_codes[:, cols], tab_codes[:].indirect(listed(cols)))
        hi1 = tile("hi32", [P, WOVEN], BF16)
        nc.vector.tensor_single_scalar(hi1[:].bitcast(I32), upper[:].bitcast(I32), HI_MASK_PAIR, ALU.bitwise_and)

        keep = {}

        def gate_tanh(u, cols, bank, name):
            ga = ps.tile([P, HALF], F32, name=bank)
            nc.tensor.matmul_mx(
                out=ga[:],
                lhsT=wg_codes[:, 2 * u * P : 2 * (u + 1) * P].bitcast(FP4X4),
                lhsT_scale=wg_plane[:, u * P : (u + 1) * P],
                rhs=v_codes[:, cols].bitcast(FP8X4),
                rhs_scale=v_plane[:, cols],
                start=True,
                stop=True,
            )
            tanh = tile(name, [P, HALF], F32)
            nc.scalar.activation(tanh[:], ga[:], ACT.Tanh, bias=half_bias[:, u : u + 1], scale=0.5)
            return tanh

        def keep_of(u, cols, tanh, name=None):
            half = cols.start // HALF
            keep[u, half] = tile(name or "keep%d%d" % (u, half), [P, HALF], F32)
            nc.scalar.activation(keep[u, half][:], tanh[:], ACT.Identity, bias=0.5, scale=-0.5)

        def kept(u, cols):
            half = cols.start // HALF
            return keep[u, half][:, cols.start - half * HALF : cols.stop - half * HALF]

        def transform(parts, bank):
            ha = ps.tile([P, J], F32, name=bank)
            for part, (codes, plane) in enumerate(parts):
                nc.tensor.matmul_mx(
                    out=ha[:],
                    lhsT=codes.bitcast(FP8X4),
                    lhsT_scale=plane,
                    rhs=v_codes[:].bitcast(FP8X4),
                    rhs_scale=v_plane[:],
                    start=(part == 0),
                    stop=(part == 1),
                )
            return ha

        def gelu_of(ha, cols, gelu):
            nc.scalar.activation(gelu, ha[:, cols], ACT.Gelu_apprx_tanh, bias=gelu_bias[:])
            return gelu

        def carry(u, cols, into):
            nc.vector.tensor_tensor(into, r_rows[u][:].indirect(listed(cols)), kept(u, cols), ALU.mult)

        result = per_row_tile("result", [P, J], F32)

        def make(u, cols, gelu):
            made = tile("made%d%d" % (u, cols.start // HALF), [P, HALF], F32)
            nc.vector.scalar_tensor_tensor(made[:], kept(u, cols), 1.0, gelu, ALU.subtract, ALU.mult)
            return made

        def finish(u, cols, carried, made):
            nc.vector.tensor_tensor(result[u][:, cols], carried, made, ALU.subtract)
            nc.sync.dma_start(out=out[u * P : (u + 1) * P, cols], in_=result[u][:, cols])

        tanh0a = gate_tanh(0, first, "bank0", "tanh0a")
        tanh1a = gate_tanh(1, first, "bank1", "tanh1a")
        keep_of(0, first, tanh0a)
        keep_of(1, first, tanh1a)
        tanh0b = gate_tanh(0, second, "bank2", "tanh0a")
        tanh1b = gate_tanh(1, second, "bank3", "tanh1a")
        keep_of(0, second, tanh0b)

        quantise(codes0[:], plane0[:], staging[:])
        ha0 = transform([(codes0[:, c], plane0[:, c]) for c in (slice(0, P), slice(P, 2 * P))], "bank0")
        both = tile("tanh0a", [P, J], F32)
        gelu0 = [gelu_of(ha0, cols, both[:, cols]) for cols in halves]
        nc.vector.tensor_tensor(words_in_runs(lo1[:]), rows_in_runs(w_raw[1][:]), words_in_runs(hi1[:]), ALU.subtract)
        quantise(codes1[0][:], plane1[0][:], hi1[:])
        quantise(codes1[1][:], plane1[1][:], lo1[:])
        ha1 = transform([(codes1[part][:], plane1[part][:]) for part in range(2)], "bank2")

        carried0 = tile("w_raw1", [P, J], F32)
        carried1a = tile("w_raw0", [P, HALF], F32)
        carry(0, first, carried0[:, first])
        carry(1, first, carried1a[:])
        carry(0, second, carried0[:, second])
        made0 = [make(0, cols, gelu) for cols, gelu in zip(halves, gelu0)]
        for cols, made in zip(halves, made0):
            finish(0, cols, carried0[:, cols], made[:])

        keep_of(1, second, tanh1b, "tanh0a")
        gelu1a = gelu_of(ha1, first, tile("gelu1a", [P, HALF], F32)[:])
        gelu1b = gelu_of(ha1, second, tile("gelu1b", [P, HALF], F32)[:])
        made1a = make(1, first, gelu1a)
        made1b = make(1, second, gelu1b)
        finish(1, first, carried1a[:], made1a[:])
        carried1b = tile("gelu1a", [P, HALF], F32)
        for cols in ends:
            carry(1, cols, carried1b[:, cols.start - HALF : cols.stop - HALF])
        for cols in ends:
            part = slice(cols.start - HALF, cols.stop - HALF)
            finish(1, cols, carried1b[:, part], made1b[:, part])
